import numpy as np, ml_dtypes
CORES = [25,29,65,69,153,157,193,197]
N = 8
import mx_ref
BF = ml_dtypes.bfloat16
def gcols(t, e):
    v = np.concatenate([t.reshape(8, 16, -1, 4), np.zeros((8, 16, 1, 4), BF)], axis=2)
    return np.ascontiguousarray(np.stack([v[g][:, e[g]] for g in range(8)])).reshape(128, -1)
def gpick(z, e):
    return np.concatenate([z[16 * g:16 * g + 16][:, e[g]] for g in range(8)])
def pick(q, e):
    c = np.concatenate([q[0].reshape(128, -1, 4), np.zeros((128, 1, 4), np.uint8)], axis=1); s = np.concatenate([q[1], np.ones((16, 1), np.uint8)], axis=1)
    return (np.ascontiguousarray(c[:, e].reshape(128, -1)), np.ascontiguousarray(s[:, e]))
def join(*qs):
    return (np.concatenate([q[0] for q in qs], axis=1), np.concatenate([q[1] for q in qs], axis=1))
def put(q, e, v):
    c, s = q[0].reshape(128, -1, 4).copy(), q[1].copy(); c[:, e] = v[0].reshape(128, -1, 4); s[:, e] = v[1]
    return (c.reshape(128, -1), s)
def pk(c, s):
    return (np.ascontiguousarray(c), mx_ref.live(s))
def emit(q):
    return q[0], q[1]
def packed(v, rng):
    q = [mx_ref.quantize(np.ascontiguousarray(v[r])) for r in range(N)]
    return np.stack([a for a, b in q]), np.stack([mx_ref.plane(b, rng) for a, b in q])
def values_of_codes():
    e, c = np.zeros((128, 128, 4), np.float32), np.zeros((128, 2, 4), np.uint8)
    e[np.arange(128), np.arange(128), 0] = 1
    c[:127, :, 0] = np.arange(256).reshape(2, 128).T[:127]
    return mx_ref.matmul(mx_ref.quantize(e.reshape(128, 512).astype(BF)), (c.reshape(128, 8), np.full((16, 2), 127, np.uint8))).T.reshape(-1).astype(np.float64)
CODE_VALUE, SCALE_VALUE = values_of_codes(), 2.0 ** (np.arange(256) - 127.0)
def decode(q):
    return (CODE_VALUE[q[0]].reshape(16, 8, -1, 4) * SCALE_VALUE[q[1]][:, None, :, None] + 0.0).reshape(128, -1).astype(np.float32)
def f(rng, *shape):
    return mx_ref.flush((rng.standard_normal(shape, dtype=np.float32) * np.exp2(rng.integers(-2, 3, shape[:-1] + (1,)))).astype(BF))
def wide(rng, *shape, cols=0):
    v = rng.standard_normal(shape, dtype=np.float32) * np.exp2(rng.integers(-12, 13, shape)).astype(np.float32)
    if cols: v *= np.repeat(np.exp2(rng.integers(-cols, cols + 1, shape[:-2] + (1, shape[-1] // 4))) * (rng.random(shape[:-2] + (1, shape[-1] // 4)) > 0.0625), 4, axis=-1).astype(np.float32)
    return mx_ref.flush(v.astype(BF))
C, R = 224, 3
DECIDE = np.flatnonzero(np.arange(128) % 16 < 8)
def partner(r, t):
    return r ^ (1 << t)
def parents(s):
    b = np.packbits(s.reshape(8 * N, 16, C)[:, :8] > 0, axis=1, bitorder="little")[:, 0].astype(np.int64)
    return b * np.arange(C) >> 8
def places(p):
    i, size = np.arange(len(p)), np.ones(p.shape, np.int64)
    for j in range(C - 1, 0, -1): size[i, p[:, j]] += size[:, j]
    place, free = np.zeros(p.shape, np.int64), np.ones(p.shape, np.int64)
    for j in range(1, C):
        place[:, j] = free[i, p[:, j]]
        free[i, p[:, j]] += size[:, j]
        free[:, j] = place[:, j] + 1
    return place
def highest(h, p):
    i = np.arange(len(p))
    for j in range(C - 1, 0, -1):
        k = p[:, j]
        h[i, :, k] = np.maximum(h[i, :, k], h[:, :, j])
    return h
def numbers_of(rng):
    return {"x": np.array(f(rng, N, 128, 4 * C)), "u": np.array(f(rng, N, 128, 512)), "v": np.array(f(rng, N, 128, 512))}
def weights(rng, w):
    c, p = packed(w, rng)
    return {"wc": c, "ws": p}
def setup_inputs(rng):
    return {**numbers_of(rng), **weights(rng, f(rng, N, 128, 2048))}
def setup_inputs_trees(rng):
    d = numbers_of(rng)
    x = d["x"].astype(np.float32).reshape(N, 8, 16, C, 4)
    w = np.array(f(rng, N, 128, 2048)).astype(np.float32).reshape(N, 8, 16, 4, 8, 16, 4)
    u = d["u"].reshape(N, 128, 128, 4)
    low = rng.permutation(N) < N // 2
    size, one = np.where(low, 2.0 ** -28, 1.0), np.where(low, 2.0 ** -30, 1.0)
    x[:, :, :8] = 0
    x[:, :, 8, :, 0] = 1
    w[:, :, :, :, :, :9] = 0
    for r in range(N):
        for g, k in enumerate(rng.permutation(8)):
            way = -1.0 if k == 1 or k == 3 and r % 2 else 1.0
            a = np.full((8, C), (-0.75, -0.75, 1.0, 0.0, 0.0, -4.0, 1.0, -1.0)[k])
            if k == 3: a = rng.choice([1.0, -0.75, -1.0, -4.0], (8, C))
            if k == 5: a[7] = 1
            if k == 6: a[0] = rng.choice([1.0, -4.0], C)
            x[r, g, :8, :, 0] = way * a * size[r]
            w[r, g, 8, 0, g, :8, 0] = 32 * way * size[r]
    u[:, :, DECIDE] = 0
    u[:, DECIDE, DECIDE, 0] = one.astype(np.float32).astype(BF)[:, None]
    return {"x": x.reshape(N, 128, 4 * C).astype(BF), "u": u.reshape(N, 128, 512), "v": d["v"], **weights(rng, w.reshape(N, 128, 2048).astype(BF))}
def setup_inputs_zeros(rng):
    d = numbers_of(rng)
    x = d["x"].reshape(N, 128, C, 4)
    for r in range(N):
        a = x[r][:, :5].copy()
        a[:, :2] = 0
        x[r] = a[:, rng.permutation(C) % 5]
    x[rng.integers(N)] = 0
    return {"x": x.reshape(N, 128, 4 * C), "u": d["u"], "v": d["v"], **weights(rng, f(rng, N, 128, 2048))}
def setup_inputs_huge(rng):
    d = numbers_of(rng)
    high = int(rng.integers(N))
    size = np.full(N, 0.25)
    size[high] = 1
    x = 2.0 ** 30 * (0.5 + 0.5 * rng.random((N, 8, 16, C, 4)))
    x[:, :, :8] *= size[:, None, None, None, None]
    x[high, :, 0, :, 0] = 2.0 ** 30
    c = np.stack([rng.permutation(C) % 2 * 2.0 - 1.0 for r in range(N)])
    x[:, :, :8, :, 2:] *= c[:, None, None, :, None]
    u = d["u"].reshape(N, 8, 16, 128, 4)
    a = 2.0 ** 30 * (0.75 + 0.25 * rng.random((N, 8, 8, 64, 2))) * rng.choice([-1.0, 1.0], (N, 1, 1, 64, 1))
    u[:, :, :, DECIDE] = 0
    u[:, :, :8, DECIDE, 2:] = a.astype(np.float32).astype(BF)
    w = np.zeros((N, 8, 16, 4, 8, 16, 4), np.float32)
    for g in range(8):
        for p in range(8):
            for b in range(2): w[:, g, p, b, g, p + 8, b] = -32
    return {"x": x.astype(np.float32).reshape(N, 128, 4 * C).astype(BF), "u": u.reshape(N, 128, 512), "v": d["v"], **weights(rng, w.reshape(N, 128, 2048).astype(BF))}
def setup_inputs_spread(rng):
    d = setup_inputs(rng)
    d["x"] = wide(rng, N, 128, 4 * C, cols=6)
    return d
def check_inputs(d):
    b = []
    for k in ("x", "u", "v"):
        a = np.abs(d[k].astype(np.float32))
        if not (np.isfinite(a).all() and ((a == 0) | (a >= 2.0 ** -30) & (a <= 2.0 ** 30)).all()): b.append("a value of " + k)
    if ((d["wc"] == 127) | (d["wc"] == 255)).any(): b.append("a code of wc that is no number")
    ends = np.tile(np.repeat(np.array([0.0, 2.0 ** -30, 2.0 ** 30, 0.0]), 4), (128, 1)).astype(BF)
    none, least, most = emit(mx_ref.quantize(ends))[1][0, :3]
    s = np.stack([mx_ref.live(p) for p in d["ws"]])
    if not ((s == none) | (s >= least) & (s <= most)).all(): b.append("a scale of ws")
    return b
def reference(x, u, v, wc, ws):
    qu = [mx_ref.quantize(u[r]) for r in range(N)]
    lay = [pk(wc[r], ws[r]) for r in range(N)]
    now = x
    for t in range(R):
        held = [mx_ref.quantize(now[r]) for r in range(N)]
        own = np.stack([decode(q).astype(BF) for q in held])
        p = parents(np.stack([mx_ref.matmul(qu[r], held[r]) for r in range(N)]))
        place = places(p)
        o, place = np.argsort(place, axis=1).reshape(N, 8, C), place.reshape(N, 8, C)
        sent = [mx_ref.quantize(gcols(own[r], o[r])) for r in range(N)]
        h = np.zeros((N, 128, C, 4), np.float32)
        for r in range(N):
            for b in range(4):
                z = mx_ref.matmul(pick(lay[r], np.arange(128 * b, 128 * b + 128)), sent[partner(r, t)]) * np.float32(0.03125)
                h[r, :, :, b] = gpick(z, place[r])
        m = highest(h.reshape(8 * N, 16, C, 4), p).reshape(N, 128, 4 * C)
        now = (own.astype(np.float32) + m).astype(BF)
    y, op = np.zeros((N, 128, C), np.float32), p.reshape(N, 8, C).astype(np.float32)
    oc, osc = np.zeros((N, 128, 4 * C), np.uint8), np.zeros((N, 16, C), np.uint8)
    for r in range(N):
        q = mx_ref.quantize(now[r])
        y[r] = mx_ref.matmul(mx_ref.quantize(v[r]), q)
        oc[r], osc[r] = emit(q)
    return {"y": y, "op": op, "oc": oc, "osc": osc}

@@ -1,0 +1,556 @@
+from concourse.mybir import dt, AluOpType, AxisListType, ActivationFunctionType
+
+C, R = 224, 3
+D = 4 * C
+TRI = 1680
+BIG = 1.0e29
+MAGIC = 12582912.0
+P16, P4, HH, S4, S16, XX, YY = [k * D for k in range(7)]
+TABW = 7 * D + 32
+
+BF, F32, I32, U16, X4, U8 = "bfloat16", "float32", "int32", "uint16", "float8_e4m3fn_x4", "uint8"
+SCRATCH = {}
+
+
+def _sb(name, n, t):
+    SCRATCH[name] = ("sbuf", [128, n], t)
+
+
+for _n, _w, _t in [
+    ("xt", D, BF), ("xs", D, BF), ("ut", 512, BF), ("vt", 512, BF), ("ez", 528, BF), ("eo", 528, BF),
+    ("eq", 512, X4), ("es", 512, U8), ("uq", 128, X4), ("us", 128, U8), ("vq", 128, X4), ("vs", 128, U8),
+    ("wq", 512, X4), ("wp", 512, U8), ("fq", C, X4), ("fs", C, U8), ("tp", D, BF), ("bt", D, BF),
+    ("idp", 272, BF), ("lx", 16, U16), ("px", 48, BF), ("ci", 16, I32), ("cf", 16, F32), ("cg", 16, F32), ("cl", 8, U16),
+    ("wtb", 16, F32), ("wtm", 16, F32), ("thr", 2, F32), ("jb", 32, F32), ("d0", 480, BF),
+    ("zf", 256, BF), ("tt", 480, BF), ("to", 480, BF), ("pl16", 16, U16), ("pwb", 16, BF), ("pwf", 16, F32),
+    ("prep", C, BF), ("pout", C, F32), ("ccb", 16, BF), ("ccn", 16, F32), ("pat", 16, BF), ("pbk", 16, BF), ("pb2", 16, BF),
+    ("klc", TRI, BF), ("kps", TRI, BF), ("xlc", TRI, BF), ("xps", TRI, BF), ("olc", TRI, BF), ("ops", TRI, BF),
+    ("ex", 256, BF), ("sp0", 240, BF), ("sp1", 240, BF), ("sp2", 240, BF), ("sp3", 240, BF),
+    ("eo1", 256, BF), ("eo2", 256, BF), ("ld", 16, U16), ("lps", 16, U16), ("pt1", 16, F32), ("pt2", 16, F32),
+    ("ja", 512, BF), ("jc", 512, BF), ("bot", 480, BF), ("ol", 28, U16), ("lb", 16, U16), ("plr", C, BF), ("rr", C, BF),
+    ("z", 96, I32), ("dd", 48, I32), ("ff", 48, I32), ("th", 48, I32), ("mm", 48, I32), ("w1", 128, I32), ("lr", 48, U16),
+    ("tab", TABW, F32), ("k4", D, F32), ("k16", D, F32), ("sq", 96, BF), ("ksq", 96, F32), ("lsq", 24, U16),
+    ("mseq", 384, F32), ("ga", D, F32), ("gb", D, F32), ("gm", D, F32), ("yo", C, F32),
+]:
+    _sb(_n, _w, _t)
+for _k in range(R + 1):
+    _sb("qx%d" % _k, C, X4)
+    _sb("sx%d" % _k, C, U8)
+for _k in range(R):
+    _sb("lq%d" % _k, C, X4)
+    _sb("ls%d" % _k, C, U8)
+    _sb("ll%d" % _k, 14, U16)
+SCRATCH["pt"] = ("psum", [128, 2048], F32)
+SCRATCH["ph"] = ("psum", [128, 2048], F32)
+
+SEMAPHORES = ["ev", "ea", "et", "eg"] + ["dm%d" % k for k in range(16)] + \
+    [a + b + str(k) for a in "as" for b in "qsl" for k in range(R)]
+
+
+def count(mask):
+    return bin(mask).count("1")
+
+
+def route(T, topo, rank, t):
+    src, dst = T.cores[rank], T.cores[rank ^ (1 << t)]
+    if topo.may_write(src, dst):
+        return dst, dst
+    can = [c for c in topo.cores_of(src) if T.rank_of(c) is None and topo.may_write(c, dst)]
+    return [c for c in can if topo.die(c) == topo.die(src)][0], dst
+
+
+def hand_on(g, core, T, topo):
+    for t in range(R):
+        for r in range(len(T.cores)):
+            hop, dst = route(T, topo, r, t)
+            if hop != core or hop == dst:
+                continue
+            n_in = count(topo.mask(T.cores[r], core))
+            rid, pid = topo.addr(dst, core)
+            m = topo.mask(core, dst)
+            for k, ap in (("q", T["lq%d" % t][:].bitcast(dt.uint8)), ("s", T["ls%d" % t][:]), ("l", T["ll%d" % t][:])):
+                g.wait_ge(T.sem["a%s%d" % (k, t)], n_in)
+                g.remote_dma(ap, ap, T.sem["a%s%d" % (k, t)], T.sem["s%s%d" % (k, t)], pid, rid, m)
+            for k in "qsl":
+                g.wait_ge(T.sem["s%s%d" % (k, t)], count(m))
+
+
+def rank_program(g, core, T, topo):
+    rank = T.rank_of(core)
+    if rank is None:
+        hand_on(g, core, T, topo)
+        return
+    A = AluOpType
+    AF = ActivationFunctionType
+    Q = {"v": g.vector, "a": g.scalar, "t": g.tensor, "g": g, "s": g.sync}
+    cnt = {"ev": 0, "ea": 0, "et": 0, "eg": 0}
+    known = {e: {} for e in Q}
+    clock = {}
+    recs = {}
+    totals = {}
+    ndma = [0]
+
+    def V(name, a=0, b=None, s=1):
+        w = SCRATCH[name][1][1]
+        b = w if b is None else b
+        if SCRATCH[name][0] == "psum":
+            lo, hi = a // 512 * 512, (b + 511) // 512 * 512
+            m = ((1 << (hi - lo)) - 1) << lo
+        elif abs(s) == 1:
+            m = ((1 << (b - a)) - 1) << a
+        else:
+            m = sum(1 << i for i in range(a, b, s))
+        if s == -1:
+            ap = T[name][:, b - 1:(a - 1 if a else None):-1]
+        elif s == 1:
+            ap = T[name][:, a:b]
+        else:
+            ap = T[name][:, a:b:s]
+        return (ap, name, m, [])
+
+    def IND(win, off):
+        return (win[0].indirect(off[0]), win[1], win[2], [off])
+
+    def ap(x):
+        return x[0] if isinstance(x, tuple) else x
+
+    def need(e, ev):
+        s, n = ev
+        if known[e].get(s, 0) >= n:
+            return
+        Q[e].wait_ge(T.sem[s], n)
+        for s2, n2 in clock[ev].items():
+            if known[e].get(s2, 0) < n2:
+                known[e][s2] = n2
+
+    def order(e, writes, reads):
+        rd = []
+        for x in reads:
+            if isinstance(x, tuple):
+                rd.append(x)
+                rd.extend(x[3])
+        for x in writes:
+            rd.extend(x[3])
+        wr = list(writes) + [x for x in rd if SCRATCH[x[1]][0] == "psum"]
+        rd = [x for x in rd if SCRATCH[x[1]][0] != "psum"]
+        evs = {}
+        for x in wr:
+            for m, ev, w in recs.get(x[1], []):
+                if m & x[2]:
+                    evs[ev[0]] = max(evs.get(ev[0], 0), ev[1])
+        for x in rd:
+            for m, ev, w in recs.get(x[1], []):
+                if w and m & x[2]:
+                    evs[ev[0]] = max(evs.get(ev[0], 0), ev[1])
+        for s in sorted(evs, key=lambda s: s == "e" + e):
+            need(e, (s, evs[s]))
+        return wr, rd
+
+    def note(e, ev, wr, rd):
+        clock[ev] = dict(known[e])
+        clock[ev][ev[0]] = ev[1]
+        totals[ev[0]] = ev[1]
+        for x in wr:
+            recs[x[1]] = [(m & ~x[2], v, w) for m, v, w in recs.get(x[1], []) if m & ~x[2]] + [(x[2], ev, True)]
+        for x in rd:
+            recs.setdefault(x[1], []).append((x[2], ev, False))
+
+    def op(e, writes, reads, call):
+        wr, rd = order(e, writes, reads)
+        s = "e" + e
+        cnt[s] += 1
+        call().then_inc(T.sem[s], 1)
+        note(e, (s, cnt[s]), wr, rd)
+
+    def dma(e, out, in_, writes, reads):
+        wr, rd = order(e, writes, reads)
+        s = "dm%d" % ndma[0]
+        ndma[0] += 1
+        Q[e].dma_start(out, in_).then_inc(T.sem[s], 16)
+        note(e, (s, 16), wr, rd)
+
+    def send(kind, t, src, land):
+        hop, dst = route(T, topo, rank, t)
+        wr, rd = order("g", [], [src])
+        rid, pid = topo.addr(hop, core)
+        m = topo.mask(core, hop)
+        a, b = src[0], land[0]
+        if kind == "q":
+            a, b = a.bitcast(dt.uint8), b.bitcast(dt.uint8)
+        g.remote_dma(b, a, T.sem["a%s%d" % (kind, t)], T.sem["s%s%d" % (kind, t)], pid, rid, m)
+        note("g", ("s%s%d" % (kind, t), count(m)), wr, rd)
+        hop2, me = route(T, topo, rank ^ (1 << t), t)
+        last = dst if hop2 == me else hop2
+        ev = ("a%s%d" % (kind, t), count(topo.mask(last, core)))
+        clock[ev] = {ev[0]: ev[1]}
+        totals[ev[0]] = ev[1]
+        recs[land[1]] = [(land[2], ev, True)]
+
+    def ts(out, in0, s1, o0, s2=None, o1=None):
+        if o1 is None:
+            op("v", [out], [in0, s1], lambda: g.vector.tensor_scalar(out[0], in0[0], ap(s1), None, o0))
+        else:
+            op("v", [out], [in0, s1, s2], lambda: g.vector.tensor_scalar(out[0], in0[0], ap(s1), ap(s2), o0, o1))
+
+    def tt(out, a, b, o):
+        op("v", [out], [a, b], lambda: g.vector.tensor_tensor(out[0], a[0], b[0], o))
+
+    def cp(out, a):
+        op("v", [out], [a], lambda: g.vector.tensor_copy(out[0], a[0]))
+
+    def ms(out, c):
+        op("v", [out], [], lambda: g.vector.memset(out[0], c))
+
+    def scan(out, d0, d1, init, o0, o1):
+        op("v", [out], [d0, d1], lambda: g.vector.tensor_tensor_scan(out[0], d0[0], d1[0], init, o0, o1))
+
+    def act(out, a, f=AF.Copy, scale=1.0, bias=None):
+        if bias is None:
+            op("a", [out], [a], lambda: g.scalar.activation(out[0], a[0], f, scale=scale))
+        else:
+            op("a", [out], [a, bias], lambda: g.scalar.activation(out[0], a[0], f, bias=ap(bias), scale=scale))
+
+    def quant(q, s, x):
+        op("v", [q, s], [x], lambda: g.vector.quantize_mx(q[0], s[0], x[0]))
+
+    def mm(out, lq, ls, rq, rs):
+        op("t", [out], [lq, ls, rq, rs], lambda: g.tensor.matmul_mx(out[0], lq[0], ls[0], rq[0], rs[0], True, True))
+
+    def iota(out, pat, base=0, cm=0):
+        if SCRATCH[out[1]][2] == I32:
+            op("g", [out], [], lambda: g.iota(out[0], pat, base, cm))
+        else:
+            op("g", [out], [], lambda: g.iota(out[0], pat, base, cm, allow_small_or_imprecise_dtypes=True))
+
+    def asel(out, a, pat, cmp, fill_, base, cm):
+        op("g", [out], [a], lambda: g.affine_select(out[0], a[0], pat, cmp, fill_, base, cm))
+
+    def gather2(out, o0, win, off, c0, c1, cv):
+        if cv < c1:
+            act(V(out, o0 + 16 * (cv - c0), o0 + 16 * (c1 - c0)), IND(win, V(off, cv, c1)))
+        if cv > c0:
+            cp(V(out, o0, o0 + 16 * (cv - c0)), IND(win, V(off, c0, cv)))
+
+    def diag(eo, src, a, n, k="ex"):
+        scan(V(eo, 0, n), V(src, a, a + n), V(k, 0, n), -1.0, A.max, A.add)
+
+    def pickd(out, eo, a, n):
+        ts(out, V(eo, a + 15, n, 16), 256.0, A.add)
+
+    def scores(t):
+        qx, sx = V("qx%d" % t), V("sx%d" % t)
+        quant(qx, sx, V("xt" if t == 0 else "xs"))
+        mm(V("ph", 0, C), V("uq"), V("us"), qx, sx)
+
+    later = []
+
+    def fill(n=1):
+        for k in range(min(n, len(later))):
+            later.pop(0)()
+
+    dma("s", T.xt[:], T.x[:], [V("xt")], [])
+    dma("a", T.ut[:], T.u[:], [V("ut")], [])
+    dma("s", T.wq[:].bitcast(dt.uint8), T.wc[:], [V("wq")], [])
+    dma("s", T.wp[:], T.ws[:], [V("wp")], [])
+    dma("s", T.vt[:], T.v[:], [V("vt")], [])
+
+    iota(V("ci", 0, 1), [[0, 1]], 0, 1)
+    iota(V("idp"), [[1, 272]])
+    iota(V("jb", 0, 14), [[32, 7], [0, 2]])
+    iota(V("jb", 14, 30), [[32, 8], [0, 2]], -16)
+    iota(V("kps"), [[0, TRI]], -1)
+    ms(V("d0"), 0.5)
+    ms(V("zf"), 0.0)
+    ms(V("wtb", 0, 8), 128.0)
+    ms(V("wtb", 8, 9), -127.5 / 256)
+    ms(V("wtb", 9, 10), MAGIC)
+    ms(V("wtb", 10, 11), -MAGIC)
+    ms(V("wtb", 11, 13), 256.0)
+    ms(V("wtb", 13, 16), 0.0)
+    p = V("ci", 0, 1)
+    ts(V("ci", 1, 2), p, 15, A.bitwise_and)
+    ts(V("ci", 2, 3), p, 31, A.bitwise_and)
+    ts(V("ci", 3, 4), p, 4, A.logical_shift_right)
+    ms(V("d0", 0, 480, 16), 0.0)
+    tt(V("ci", 4, 5), p, V("ci", 3, 4), A.add)
+    ms(V("d0", 9, 480, 16), 1.0)
+    ts(V("ci", 5, 6), V("ci", 4, 5), 1, A.bitwise_and)
+    ms(V("d0", 10, 480, 16), 1.0)
+    cp(V("cf", 0, 6), V("ci", 0, 6))
+    ms(V("d0", 11, 480, 16), -1.0)
+    pm16, pm32, par = V("cf", 1, 2), V("cf", 2, 3), V("cf", 5, 6)
+    ts(V("pat"), V("idp", 0, 16), pm16, A.max)
+    ts(V("pb2"), V("idp", 0, 16), pm16, A.add, 15.5, A.is_le)
+    ts(V("wtm"), V("idp", 0, 16), pm16, A.is_equal)
+    ts(V("thr", 0, 1), pm16, 7.5, A.is_gt, -BIG, A.mult)
+    ts(V("pbk"), V("pb2"), 1025.0, A.mult, -1.0, A.add)
+    tt(V("wtm"), V("wtm"), V("wtb"), A.mult)
+    ts(V("d0", 8, 480, 16), V("jb", 0, 30), pm32, A.add, 1.0 / 256, A.mult)
+    op("v", [V("thr", 1, 2)], [V("wtm")], lambda: g.vector.tensor_reduce(T.thr[:, 1:2], T.wtm[:], AxisListType.X, A.add))
+    ts(V("cg", 0, 1), pm16, 16.0, A.mult, 12.0, A.add)
+    ts(V("cg", 1, 2), pm16, -1.0, A.mult, 14.0, A.add)
+    ts(V("cg", 2, 3), pm16, 1.0, A.add, 14.0, A.min)
+    ts(V("ccb", 0, 14), V("idp", 0, C, 16), pm16, A.add)
+    quant(V("uq"), V("us"), V("ut"))
+    scores(0)
+    ts(V("d0", 12, 480, 16), V("d0", 8, 480, 16), 0.0, A.not_equal, -1.0, A.mult)
+    ts(V("cg", 3, 4), par, 240.0, A.mult, V("cg", 0, 1), A.add)
+    ts(V("cg", 1, 2), V("cg", 1, 2), 1.0, A.max)
+    ts(V("ccn", 0, 14), V("ccb", 0, 14), -512.0, A.mult)
+    ts(V("cg", 4, 6), V("cg", 1, 3), 1.0, A.add, 8.0, A.mult)
+    ts(V("cl", 0, 1), V("cg", 3, 4), 476.0, A.min)
+    tt(V("cg", 6, 8), V("cg", 4, 6), V("cg", 1, 3), A.mult)
+
+    def seg_lc(m):
+        n = 14 - m
+        return 8 * n * (n - 1), 16 * n
+
+    def seg_ps(m):
+        n = m + 1
+        return 8 * n * (n - 1), 16 * n
+
+    for m in range(14):
+        a, n = seg_lc(m)
+        if n > 16:
+            act(V("klc", a + 16, a + n), V("idp", 16 * m + 16, C), AF.Identity, -1.0, 256.0)
+    for m in range(14):
+        a, n = seg_lc(m)
+        act(V("klc", a, a + 16), V("pat"), AF.Identity, -1.0, 256.0 - 16 * m)
+    for m in range(7):
+        a, n = seg_ps(m)
+        act(V("kps", a, a + 16), V("pbk"))
+
+    def late_vector_constants():
+        later.extend([
+            lambda: ts(V("px", 0, 16), V("idp", 0, 16), pm16, A.is_equal, 256.0, A.mult),
+            lambda: ts(V("px", 16, 32), V("idp", 0, 16), pm16, A.is_lt, -256.0, A.mult),
+            lambda: tt(V("px", 32, 48), V("px", 0, 16), V("px", 16, 32), A.add),
+            lambda: ts(V("lx"), V("idp", 0, 16), 0.0, A.mult, pm16, A.add),
+            lambda: ts(V("px", 47, 48), V("px", 47, 48), -512.0, A.add),
+            lambda: ts(V("cl", 2, 6, 2), V("cg", 6, 8), -1.0, A.add),
+            lambda: ms(V("lps", 0, 2), 256)])
+
+    def jump_constants():
+        for b in range(4):
+            later.append(lambda b=b: quant(V("eq", 128 * b, 128 * b + 128), V("es", 128 * b, 128 * b + 128), V("ez", 3 - b, 515 - b)))
+        for k in range(4):
+            later.append(lambda k=k: ts(V("ci", 6 + k, 7 + k), p, k, A.logical_shift_right, 1, A.bitwise_and))
+        later.append(lambda: ts(V("cg", 8, 12), V("ci", 6, 10), float(C), A.mult))
+        later.append(lambda: ms(V("ol"), 0))
+
+    def order_constants():
+        later.append(lambda: ts(V("ksq"), V("sq"), D / 16, A.is_equal, -BIG, A.mult))
+        later.append(lambda: diag("eo2", "sq", 0, 96))
+        for b in range(4):
+            later.append(lambda b=b: ts(V("lsq", 6 * b, 6 * b + 6), V("eo2", 15, 96, 16), 16.0, A.mult, 4096.0 + C * b, A.add))
+
+    def late_constants():
+        iota(V("eo"), [[0, 528]], 1)
+        asel(V("ez"), V("eo"), [[1, 528]], A.is_equal, 0.0, -3, -4)
+        iota(V("bot", 0, 256), [[1, 256]])
+        iota(V("ja", 288, 512), [[1, C]])
+        iota(V("jc", 288, 512), [[1, C]])
+        iota(V("th", 0, 28), [[-1, 2], [0, 14]], 4)
+        iota(V("pout", 0, 1), [[0, 1]])
+        iota(V("sq"), [[0, 96]], D // 16)
+        for j in range(2, 14):
+            a = j * (j - 1) // 2 + 1
+            iota(V("sq", a, a + j - 1), [[-1, j - 1]], j - 1)
+        iota(V("tab", YY, TABW), [[0, D + 32]])
+        asel(V("k16"), V("tab", YY, YY + D), [[0, D // 16], [1, 16]], A.is_gt, -BIG, 0, 0)
+        asel(V("tab", XX, YY), V("k16"), [[0, D]], A.is_gt, -BIG, 0, 0)
+        asel(V("k4"), V("k16"), [[0, C], [1, 4]], A.is_gt, -BIG, 0, 0)
+
+    for t in range(R):
+        qx, sx = V("qx%d" % t), V("sx%d" % t)
+        lq, ls, ll = V("lq%d" % t), V("ls%d" % t), V("ll%d" % t)
+        if t:
+            scores(t)
+        send("q", t, qx, lq)
+        send("s", t, sx, ls)
+        if t == 0:
+            late_constants()
+            late_vector_constants()
+        ts(V("zf", 16, 240), V("ph", 0, C), V("thr", 0, 1), A.is_gt, V("thr", 1, 2), A.mult)
+        fill()
+        op("v", [V("tt", 0, C)], [V("zf")], lambda: g.vector.transpose(T.tt[:, 0:C], T.zf[:, 16:240]))
+        op("v", [V("tt", C, 480)], [V("zf")], lambda: g.vector.transpose(T.tt[:, C:480], T.zf[:]))
+        fill()
+        scan(V("to"), V("d0"), V("tt"), 0.0, A.mult, A.add)
+        fill()
+        cp(V("pl16"), IND(V("to"), V("cl", 0, 1)))
+        fill()
+        gather2("prep", 0, V("idp"), "pl16", 0, 14, 8)
+        fill()
+        for m in range(13, 4, -1):
+            a, n = seg_lc(m)
+            act(V("xlc", a, a + n), V("prep", 16 * m, C), AF.Abs, 512.0, V("ccn", m, m + 1))
+        act(V("pwb"), IND(V("to"), V("cl", 0, 1)))
+        act(V("pwf"), IND(V("to"), V("cl", 0, 1)))
+        for m in range(4, -1, -1):
+            a, n = seg_lc(m)
+            ts(V("xlc", a, a + n), V("prep", 16 * m, C), V("ccb", m, m + 1), A.not_equal, 512.0, A.mult)
+        fill()
+        for a, b in ((720, TRI), (0, 720)):
+            scan(V("olc", a, b), V("xlc", a, b), V("klc", a, b), 0.0, A.min, A.max)
+        fill(9)
+        if t == 0:
+            act(V("ex"), IND(V("px", 32, 48), V("lx")))
+        ts(V("ld"), IND(V("olc"), V("cl", 2, 3)), -1.0, A.mult, 256.0, A.add)
+        gather2("ja", 64, V("idp"), "ld", 0, 14, 0)
+        if t == 0:
+            for m in range(7, 14):
+                a, n = seg_ps(m)
+                act(V("kps", a, a + 16), V("pbk"))
+        src, dst = "ja", "jc"
+        for k in range(3):
+            gather2(dst, 64, V(src, 64, 288), "ld", 0, 14, 0)
+            src, dst = dst, src
+        if t == R - 1:
+            act(V("pout", 1, C), V("prep", 1, C))
+            dma("s", T.op[:], T.pout[0:128:16, :], [], [V("pout")])
+        for m in range(14):
+            a, n = seg_ps(m)
+            ts(V("xps", a, a + n), V("prep", 0, n, -1), V("pwb", m, m + 1), A.not_equal, 512.0, A.mult)
+        scan(V("ops"), V("xps"), V("kps"), 1000.0, A.min, A.add)
+        ts(V("pt1"), IND(V("ops"), V("cl", 4, 5)), -1.0, A.mult, 255.0, A.add)
+        if t == 0:
+            jump_constants()
+        for lev in range(3):
+            if lev == 1:
+                for out, q, s in (("ph", lq, ls), ("pt", qx, sx)):
+                    for b in range(4):
+                        mm(V(out, 512 * b, 512 * b + C), V("eq", 128 * b, 128 * b + 128), V("es", 128 * b, 128 * b + 128), q, s)
+            diag("eo1", src, 64, C)
+            if lev:
+                fill()
+            if t == 0:
+                for k in range(lev, 4, 3):
+                    act(V("sp%d" % k, 0, 240), V("ex", 0, 240))
+            if lev == 0:
+                tt(V("pt2"), V("pt1"), V("pwf"), A.max)
+            pickd(V("ld", 0, 14), "eo1", 0, C)
+            if lev == 0:
+                cp(V("lps", 2, 16), V("pt2", 0, 14))
+            fill()
+            if t == 0 and lev == 2:
+                for k in range(4):
+                    act(V("sp%d" % k, 15, 16), V("ex", 15, 16), AF.Identity, 1.0, V("cg", 8 + k, 9 + k))
+            for k in range(3):
+                if lev == 2 and k == 2:
+                    gather2("bot", 256, V(src, 64, 288), "ld", 0, 14, 8)
+                else:
+                    gather2(dst, 64, V(src, 64, 288), "ld", 0, 14, 8)
+                    src, dst = dst, src
+                fill()
+        fill(9)
+        later.append(lambda: diag("eo2", "bot", 256, C))
+        later.append(lambda: pickd(V("lb", 0, 14), "eo2", 0, C))
+        if t == 0:
+            order_constants()
+        gather2("ja", 32, V("bot"), "lps", 0, 16, 8)
+        src, dst = "ja", "jc"
+        for k in range(4):
+            diag("eo1", src, 48, 240, "sp%d" % k)
+            act(V("tp", C * k, C * k + C), V("ph", 512 * k, 512 * k + C))
+            fill()
+            pickd(V("ol", 13, 28), "eo1", 0, 240)
+            fill()
+            gather2(dst, 32, V(src, 64, 512), "ol", 12, 28, 20)
+            src, dst = dst, src
+        diag("eo1", src, 48, 240)
+        pickd(V("ol", 13, 28), "eo1", 0, 240)
+        gather2(dst, 32, V(src, 64, 288), "ol", 12, 28, 20)
+        src, dst = dst, src
+        diag("eo1", src, 48, 240)
+        pickd(V("ol", 14, 28), "eo1", 16, 240)
+        pickd(V("ol", 12, 13), "eo1", 0, 16)
+        gather2(dst, 32, V(src, 64, 288), "ol", 12, 28, 20)
+        src, dst = dst, src
+        diag("eo1", src, 32, 256)
+        pickd(V("ol", 14, 28), "eo1", 32, 256)
+        pickd(V("ol", 10, 12), "eo1", 0, 32)
+        gather2(dst, 0, V(src, 64, 288), "ol", 10, 28, 18)
+        src, dst = dst, src
+        diag("eo1", src, 0, 64)
+        pickd(V("ol", 6, 10), "eo1", 0, 64)
+        gather2(dst, 64, V(src, 64, 288), "ol", 8, 14, 14)
+        diag("eo1", dst, 64, 96)
+        pickd(V("ol", 0, 6), "eo1", 0, 96)
+        send("l", t, V("ol", 0, 14), ll)
+        cp(IND(V("plr"), V("ol", 0, 14)), V("idp", 0, C))
+        act(V("rr"), IND(V("plr"), V("lb", 0, 14)))
+        diag("eo1", "plr", 0, C)
+        pickd(V("z", 56, 84, 2), "eo1", 0, C)
+        if t == 1:
+            quant(V("vq"), V("vs"), V("vt"))
+        diag("eo2", "rr", 0, C)
+        pickd(V("z", 57, 84, 2), "eo2", 0, C)
+        l, r, l4, i16, j16 = V("z", 56, 84, 2), V("z", 57, 84, 2), V("z", 28, 56, 2), V("z", 0, 28, 2), V("z", 1, 28, 2)
+        w = [V("w1", 16 * k, 16 * k + 14) for k in range(8)]
+        ts(V("z", 28, 56), V("z", 56, 84), 2, A.logical_shift_right)
+        ts(V("z", 0, 28), V("z", 56, 84), 4, A.logical_shift_right)
+        ts(w[0], l4, 4.0, A.mult, float(XX - HH + 4), A.add)
+        tt(V("dd", 0, 42), V("z", 1, 84, 2), V("z", 0, 84, 2), A.subtract)
+        ts(w[1], j16, 1.0, A.add)
+        ts(w[3], V("dd", 14, 28), -1.0, A.add, 0.0, A.max)
+        ts(w[2], i16, -2.0, A.mult, float(YY - HH - 2), A.add)
+        tt(V("dd", 14, 28), V("dd", 14, 28), V("dd", 0, 14), A.add)
+        ts(w[4], V("dd", 28, 42), 1.0, A.min)
+        tt(V("ff", 0, 28), V("dd", 14, 42), V("th", 0, 28), A.is_ge)
+        tt(w[1], w[1], j16, A.mult)
+        tt(w[5], V("ff", 0, 14), V("ff", 14, 28), A.add)
+        nv = 2 if route(T, topo, rank, t)[0] != route(T, topo, rank, t)[1] else 1
+        for b in range(nv, 4):
+            act(V("bt", b, D, 4), IND(V("tp", C * b, C * b + C), ll))
+        for b in range(nv):
+            cp(V("bt", b, D, 4), IND(V("tp", C * b, C * b + C), ll))
+        quant(V("fq"), V("fs"), V("bt"))
+        for b in range(4):
+            mm(V("ph", 512 * b, 512 * b + C), V("wq", 128 * b, 128 * b + 128), V("wp", 128 * b, 128 * b + 128), V("fq"), V("fs"))
+        for b in range(4):
+            act(V("tab", HH + C * b, HH + C * b + C), V("ph", 512 * b, 512 * b + C), AF.Copy, 0.03125)
+        ts(w[5], w[5], float(D), A.mult)
+        tt(V("mm", 14, 28), w[0], w[3], A.add)
+        tt(V("mm", 0, 14), w[1], w[2], A.add)
+        tt(w[4], w[4], l, A.add)
+        tt(w[6], l, w[5], A.add)
+        tt(w[7], r, w[5], A.subtract)
+        tt(V("dd", 0, 28), V("ff", 0, 28), V("mm", 0, 28), A.mult)
+        cp(V("lr", 0, 14), w[6])
+        tt(w[4], w[4], V("dd", 0, 14), A.max)
+        ts(V("lr", 16, 30), w[7], float(HH), A.add)
+        tt(w[4], w[4], V("dd", 14, 28), A.max)
+        for b in range(4):
+            scan(V("tab", S16 + C * b, S16 + C * b + C, -1), V("k16", 0, C), V("tab", HH + C * b, HH + C * b + C, -1), 0.0, A.add, A.max)
+            if b == 0:
+                cp(V("lr", 32, 46), w[4])
+        act(V("mseq"), IND(V("tab", S16, YY), V("lsq")))
+        scan(V("tab", S4, S16, -1), V("k4"), V("tab", HH, S4, -1), 0.0, A.add, A.max)
+        act(V("tab", XX + 1, YY, 4), V("tab", S4, S16, 4))
+        for b in range(4):
+            act(V("ga", C * b, C * b + C), IND(V("tab", HH + C * b, S16 + C * b + C), V("lr", 0, 14)))
+        scan(V("tab", P16, P4), V("k16"), V("tab", HH, S4), 0.0, A.add, A.max)
+        scan(V("tab", P4, HH), V("k4"), V("tab", HH, S4), 0.0, A.add, A.max)
+        tt(V("tab", XX + 6, YY, 16), V("tab", S4 + 4, S16, 16), V("tab", S4 + 8, S16, 16), A.max)
+        for b in range(4):
+            scan(V("tab", YY + C * b, YY + C * b + 192, 2), V("ksq"), V("mseq", 96 * b, 96 * b + 96), 0.0, A.add, A.max)
+        for b in range(4):
+            tt(V("gb", C * b, C * b + C), IND(V("tab", C * b, HH + C * b + C), V("lr", 16, 30)), V("ga", C * b, C * b + C), A.max)
+        for b in range(4):
+            tt(V("gm", C * b, C * b + C), IND(V("tab", HH + C * b, YY + C * b + C), V("lr", 32, 46)), V("gb", C * b, C * b + C), A.max)
+        for b in range(4):
+            tt(V("xs", b, D, 4), V("gm", C * b, C * b + C), V("pt", 512 * b, 512 * b + C), A.add)
+
+    qx, sx = V("qx%d" % R), V("sx%d" % R)
+    quant(qx, sx, V("xs"))
+    mm(V("ph", 0, C), V("vq"), V("vs"), qx, sx)
+    dma("s", T.oc[:], qx[0].bitcast(dt.uint8), [], [qx])
+    cp(V("yo"), V("ph", 0, C))
+    dma("a", T.osc[0:4, :], T["sx%d" % R][0:4, :], [], [sx])
+    dma("a", T.osc[4:8, :], T["sx%d" % R][32:36, :], [], [sx])
+    dma("s", T.y[:], T.yo[:], [], [V("yo")])
+    dma("a", T.osc[8:12, :], T["sx%d" % R][64:68, :], [], [sx])
+    dma("a", T.osc[12:16, :], T["sx%d" % R][96:100, :], [], [sx])
+    for s in totals:
+        need("g", (s, totals[s]))

@@ -25,9 +25,10 @@ for _n, _w, _t in [
     ("zf", 256, BF), ("tt", 480, BF), ("to", 480, BF), ("pl16", 16, U16), ("pwb", 16, BF), ("pwf", 16, F32),
     ("prep", C, BF), ("pout", C, F32), ("ccb", 16, BF), ("ccn", 16, F32), ("pat", 16, BF), ("pbk", 16, BF), ("pb2", 16, BF),
     ("klc", TRI, BF), ("kps", TRI, BF), ("xlc", TRI, BF), ("xps", TRI, BF), ("olc", TRI, BF), ("ops", TRI, BF),
-    ("ex", 256, BF), ("sp0", 240, BF), ("sp1", 240, BF), ("sp2", 240, BF), ("sp3", 240, BF),
-    ("eo1", 256, BF), ("eo2", 256, BF), ("ld", 16, U16), ("lps", 16, U16), ("pt1", 16, F32), ("pt2", 16, F32),
-    ("ja", 512, BF), ("jc", 512, BF), ("bot", 480, BF), ("ol", 28, U16), ("lb", 16, U16), ("plr", C, BF), ("rr", C, BF),
+    ("ex", 256, BF), ("eo1", 256, BF), ("eo2", 256, BF), ("eo3", 256, BF),
+    ("ld", 32, U16), ("lps", 16, U16), ("pt1", 16, F32), ("pt2", 16, F32),
+    ("ja", 512, BF), ("jc", 512, BF), ("bot", 480, BF), ("ol", 14, U16), ("oq", 32, U16), ("ot", 240, BF),
+    ("lb", 16, U16), ("plr", C, BF), ("rr", C, BF),
     ("z", 96, I32), ("dd", 48, I32), ("ff", 48, I32), ("th", 48, I32), ("mm", 48, I32), ("w1", 128, I32), ("lr", 48, U16),
     ("tab", TABW, F32), ("k4", D, F32), ("k16", D, F32), ("sq", 96, BF), ("ksq", 96, F32), ("lsq", 24, U16),
     ("mseq", 384, F32), ("ga", D, F32), ("gb", D, F32), ("gm", D, F32), ("yo", C, F32),
@@ -231,8 +232,8 @@ def rank_program(g, core, T, topo):
         if cv > c0:
             cp(V(out, o0, o0 + 16 * (cv - c0)), IND(win, V(off, c0, cv)))
 
-    def diag(eo, src, a, n, k="ex"):
-        scan(V(eo, 0, n), V(src, a, a + n), V(k, 0, n), -1.0, A.max, A.add)
+    def diag(eo, src, a, n):
+        scan(V(eo, 0, n), V(src, a, a + n), V("ex", 0, n), -1.0, A.max, A.add)
 
     def pickd(out, eo, a, n):
         ts(out, V(eo, a + 15, n, 16), 256.0, A.add)
@@ -259,47 +260,48 @@ def rank_program(g, core, T, topo):
     iota(V("jb", 0, 14), [[32, 7], [0, 2]])
     iota(V("jb", 14, 30), [[32, 8], [0, 2]], -16)
     iota(V("kps"), [[0, TRI]], -1)
+    p = V("ci", 0, 1)
     ms(V("d0"), 0.5)
     ms(V("zf"), 0.0)
-    ms(V("wtb", 0, 8), 128.0)
-    ms(V("wtb", 8, 9), -127.5 / 256)
-    ms(V("wtb", 9, 10), MAGIC)
-    ms(V("wtb", 10, 11), -MAGIC)
-    ms(V("wtb", 11, 13), 256.0)
-    ms(V("wtb", 13, 16), 0.0)
-    p = V("ci", 0, 1)
     ts(V("ci", 1, 2), p, 15, A.bitwise_and)
     ts(V("ci", 2, 3), p, 31, A.bitwise_and)
     ts(V("ci", 3, 4), p, 4, A.logical_shift_right)
-    ms(V("d0", 0, 480, 16), 0.0)
+    ms(V("wtb", 0, 8), 128.0)
+    ms(V("wtb", 8, 9), -127.5 / 256)
+    ms(V("wtb", 9, 10), MAGIC)
     tt(V("ci", 4, 5), p, V("ci", 3, 4), A.add)
-    ms(V("d0", 9, 480, 16), 1.0)
+    ms(V("wtb", 10, 11), -MAGIC)
+    ms(V("wtb", 11, 13), 256.0)
+    ms(V("wtb", 13, 16), 0.0)
     ts(V("ci", 5, 6), V("ci", 4, 5), 1, A.bitwise_and)
+    ms(V("d0", 0, 480, 16), 0.0)
+    ms(V("d0", 9, 480, 16), 1.0)
     ms(V("d0", 10, 480, 16), 1.0)
     cp(V("cf", 0, 6), V("ci", 0, 6))
     ms(V("d0", 11, 480, 16), -1.0)
     pm16, pm32, par = V("cf", 1, 2), V("cf", 2, 3), V("cf", 5, 6)
     ts(V("pat"), V("idp", 0, 16), pm16, A.max)
-    ts(V("pb2"), V("idp", 0, 16), pm16, A.add, 15.5, A.is_le)
     ts(V("wtm"), V("idp", 0, 16), pm16, A.is_equal)
+    ts(V("pb2"), V("idp", 0, 16), pm16, A.add, 15.5, A.is_le)
     ts(V("thr", 0, 1), pm16, 7.5, A.is_gt, -BIG, A.mult)
-    ts(V("pbk"), V("pb2"), 1025.0, A.mult, -1.0, A.add)
-    tt(V("wtm"), V("wtm"), V("wtb"), A.mult)
     ts(V("d0", 8, 480, 16), V("jb", 0, 30), pm32, A.add, 1.0 / 256, A.mult)
-    op("v", [V("thr", 1, 2)], [V("wtm")], lambda: g.vector.tensor_reduce(T.thr[:, 1:2], T.wtm[:], AxisListType.X, A.add))
+    tt(V("wtm"), V("wtm"), V("wtb"), A.mult)
+    ts(V("pbk"), V("pb2"), 1025.0, A.mult, -1.0, A.add)
     ts(V("cg", 0, 1), pm16, 16.0, A.mult, 12.0, A.add)
     ts(V("cg", 1, 2), pm16, -1.0, A.mult, 14.0, A.add)
-    ts(V("cg", 2, 3), pm16, 1.0, A.add, 14.0, A.min)
-    ts(V("ccb", 0, 14), V("idp", 0, C, 16), pm16, A.add)
+    op("v", [V("thr", 1, 2)], [V("wtm")], lambda: g.vector.tensor_reduce(T.thr[:, 1:2], T.wtm[:], AxisListType.X, A.add))
     quant(V("uq"), V("us"), V("ut"))
     scores(0)
+    ts(V("cg", 2, 3), pm16, 1.0, A.add, 14.0, A.min)
+    ts(V("ccb", 0, 14), V("idp", 0, C, 16), pm16, A.add)
+    ts(V("cg", 1, 2), V("cg", 1, 2), 1.0, A.max)
     ts(V("d0", 12, 480, 16), V("d0", 8, 480, 16), 0.0, A.not_equal, -1.0, A.mult)
     ts(V("cg", 3, 4), par, 240.0, A.mult, V("cg", 0, 1), A.add)
-    ts(V("cg", 1, 2), V("cg", 1, 2), 1.0, A.max)
     ts(V("ccn", 0, 14), V("ccb", 0, 14), -512.0, A.mult)
     ts(V("cg", 4, 6), V("cg", 1, 3), 1.0, A.add, 8.0, A.mult)
+    ts(V("px", 0, 16), V("idp", 0, 16), pm16, A.is_equal, 256.0, A.mult)
     ts(V("cl", 0, 1), V("cg", 3, 4), 476.0, A.min)
-    tt(V("cg", 6, 8), V("cg", 4, 6), V("cg", 1, 3), A.mult)
+    ts(V("px", 16, 32), V("idp", 0, 16), pm16, A.is_lt, -256.0, A.mult)
 
     def seg_lc(m):
         n = 14 - m
@@ -316,40 +318,34 @@ def rank_program(g, core, T, topo):
     for m in range(14):
         a, n = seg_lc(m)
         act(V("klc", a, a + 16), V("pat"), AF.Identity, -1.0, 256.0 - 16 * m)
-    for m in range(7):
+    for m in range(14):
         a, n = seg_ps(m)
         act(V("kps", a, a + 16), V("pbk"))
 
     def late_vector_constants():
         later.extend([
-            lambda: ts(V("px", 0, 16), V("idp", 0, 16), pm16, A.is_equal, 256.0, A.mult),
-            lambda: ts(V("px", 16, 32), V("idp", 0, 16), pm16, A.is_lt, -256.0, A.mult),
             lambda: tt(V("px", 32, 48), V("px", 0, 16), V("px", 16, 32), A.add),
-            lambda: ts(V("lx"), V("idp", 0, 16), 0.0, A.mult, pm16, A.add),
+            lambda: tt(V("cg", 6, 8), V("cg", 4, 6), V("cg", 1, 3), A.mult),
             lambda: ts(V("px", 47, 48), V("px", 47, 48), -512.0, A.add),
+            lambda: ts(V("lx"), V("idp", 0, 16), 0.0, A.mult, pm16, A.add),
             lambda: ts(V("cl", 2, 6, 2), V("cg", 6, 8), -1.0, A.add),
             lambda: ms(V("lps", 0, 2), 256)])
 
     def jump_constants():
         for b in range(4):
             later.append(lambda b=b: quant(V("eq", 128 * b, 128 * b + 128), V("es", 128 * b, 128 * b + 128), V("ez", 3 - b, 515 - b)))
-        for k in range(4):
-            later.append(lambda k=k: ts(V("ci", 6 + k, 7 + k), p, k, A.logical_shift_right, 1, A.bitwise_and))
-        later.append(lambda: ts(V("cg", 8, 12), V("ci", 6, 10), float(C), A.mult))
-        later.append(lambda: ms(V("ol"), 0))
+        later.append(lambda: ms(V("ot"), 0.0))
 
     def order_constants():
         later.append(lambda: ts(V("ksq"), V("sq"), D / 16, A.is_equal, -BIG, A.mult))
-        later.append(lambda: diag("eo2", "sq", 0, 96))
+        later.append(lambda: diag("eo3", "sq", 0, 96))
         for b in range(4):
-            later.append(lambda b=b: ts(V("lsq", 6 * b, 6 * b + 6), V("eo2", 15, 96, 16), 16.0, A.mult, 4096.0 + C * b, A.add))
+            later.append(lambda b=b: ts(V("lsq", 6 * b, 6 * b + 6), V("eo3", 15, 96, 16), 16.0, A.mult, 4096.0 + C * b, A.add))
 
     def late_constants():
         iota(V("eo"), [[0, 528]], 1)
         asel(V("ez"), V("eo"), [[1, 528]], A.is_equal, 0.0, -3, -4)
         iota(V("bot", 0, 256), [[1, 256]])
-        iota(V("ja", 288, 512), [[1, C]])
-        iota(V("jc", 288, 512), [[1, C]])
         iota(V("th", 0, 28), [[-1, 2], [0, 14]], 4)
         iota(V("pout", 0, 1), [[0, 1]])
         iota(V("sq"), [[0, 96]], D // 16)
@@ -381,104 +377,109 @@ def rank_program(g, core, T, topo):
         cp(V("pl16"), IND(V("to"), V("cl", 0, 1)))
         fill()
         gather2("prep", 0, V("idp"), "pl16", 0, 14, 8)
-        fill()
+        fill(9)
         for m in range(13, 4, -1):
             a, n = seg_lc(m)
             act(V("xlc", a, a + n), V("prep", 16 * m, C), AF.Abs, 512.0, V("ccn", m, m + 1))
         act(V("pwb"), IND(V("to"), V("cl", 0, 1)))
         act(V("pwf"), IND(V("to"), V("cl", 0, 1)))
+        if t == 0:
+            act(V("ex"), IND(V("px", 32, 48), V("lx")))
         for m in range(4, -1, -1):
             a, n = seg_lc(m)
             ts(V("xlc", a, a + n), V("prep", 16 * m, C), V("ccb", m, m + 1), A.not_equal, 512.0, A.mult)
-        fill()
         for a, b in ((720, TRI), (0, 720)):
             scan(V("olc", a, b), V("xlc", a, b), V("klc", a, b), 0.0, A.min, A.max)
-        fill(9)
-        if t == 0:
-            act(V("ex"), IND(V("px", 32, 48), V("lx")))
-        ts(V("ld"), IND(V("olc"), V("cl", 2, 3)), -1.0, A.mult, 256.0, A.add)
-        gather2("ja", 64, V("idp"), "ld", 0, 14, 0)
-        if t == 0:
-            for m in range(7, 14):
-                a, n = seg_ps(m)
-                act(V("kps", a, a + 16), V("pbk"))
-        src, dst = "ja", "jc"
-        for k in range(3):
-            gather2(dst, 64, V(src, 64, 288), "ld", 0, 14, 0)
-            src, dst = dst, src
-        if t == R - 1:
-            act(V("pout", 1, C), V("prep", 1, C))
-            dma("s", T.op[:], T.pout[0:128:16, :], [], [V("pout")])
         for m in range(14):
             a, n = seg_ps(m)
-            ts(V("xps", a, a + n), V("prep", 0, n, -1), V("pwb", m, m + 1), A.not_equal, 512.0, A.mult)
-        scan(V("ops"), V("xps"), V("kps"), 1000.0, A.min, A.add)
-        ts(V("pt1"), IND(V("ops"), V("cl", 4, 5)), -1.0, A.mult, 255.0, A.add)
+            later.append(lambda a=a, n=n, m=m: ts(V("xps", a, a + n), V("prep", 0, n, -1), V("pwb", m, m + 1), A.not_equal, 512.0, A.mult))
+        for m0, m1 in ((0, 7), (7, 10), (10, 12), (12, 14)):
+            a, b = seg_ps(m0)[0], seg_ps(m1)[0]
+            later.append(lambda a=a, b=b: scan(V("ops", a, b), V("xps", a, b), V("kps", a, b), 1000.0, A.min, A.add))
+        later.append(lambda: ts(V("pt1"), IND(V("ops"), V("cl", 4, 5)), -1.0, A.mult, 255.0, A.add))
+        later.append(lambda: tt(V("pt2"), V("pt1"), V("pwf"), A.max))
+        later.append(lambda: cp(V("lps", 2, 16), V("pt2", 0, 14)))
         if t == 0:
             jump_constants()
-        for lev in range(3):
-            if lev == 1:
-                for out, q, s in (("ph", lq, ls), ("pt", qx, sx)):
-                    for b in range(4):
-                        mm(V(out, 512 * b, 512 * b + C), V("eq", 128 * b, 128 * b + 128), V("es", 128 * b, 128 * b + 128), q, s)
-            diag("eo1", src, 64, C)
-            if lev:
-                fill()
-            if t == 0:
-                for k in range(lev, 4, 3):
-                    act(V("sp%d" % k, 0, 240), V("ex", 0, 240))
-            if lev == 0:
-                tt(V("pt2"), V("pt1"), V("pwf"), A.max)
-            pickd(V("ld", 0, 14), "eo1", 0, C)
-            if lev == 0:
-                cp(V("lps", 2, 16), V("pt2", 0, 14))
-            fill()
-            if t == 0 and lev == 2:
-                for k in range(4):
-                    act(V("sp%d" % k, 15, 16), V("ex", 15, 16), AF.Identity, 1.0, V("cg", 8 + k, 9 + k))
-            for k in range(3):
-                if lev == 2 and k == 2:
-                    gather2("bot", 256, V(src, 64, 288), "ld", 0, 14, 8)
-                else:
-                    gather2(dst, 64, V(src, 64, 288), "ld", 0, 14, 8)
-                    src, dst = dst, src
-                fill()
-        fill(9)
-        later.append(lambda: diag("eo2", "bot", 256, C))
-        later.append(lambda: pickd(V("lb", 0, 14), "eo2", 0, C))
+        fill(2)
+        ts(V("ld", 0, 16), IND(V("olc"), V("cl", 2, 3)), -1.0, A.mult, 256.0, A.add)
+        fill(2)
+        gather2("ja", 64, V("idp"), "ld", 0, 14, 8)
+        fill(2)
+        gather2("jc", 64, V("ja", 64, 288), "ld", 0, 14, 8)
+        fill(2)
+        old, new = 0, 16
+        for lev in range(5):
+            gather2("ja", 64, V("jc", 64, 288), "ld", old, old + 14, old)
+            diag("eo1", "jc", 64, C)
+            fill(2 if lev < 1 else 1)
+            pickd(V("ld", new, new + 14), "eo1", 0, C)
+            fill(2 if lev < 1 else 1)
+            if t == R - 1 and lev == 0:
+                act(V("pout", 1, C), V("prep", 1, C))
+                dma("s", T.op[:], T.pout[0:128:16, :], [], [V("pout")])
+            gather2("jc", 64, V("ja", 64, 288), "ld", new, new + 14, new + 8)
+            fill(2 if lev < 1 else 1)
+            old, new = new, old
+        gather2("bot", 256, V("jc", 64, 288), "ld", old, old + 14, old + 8)
+        fill(30)
+        for out, q, s in (("ph", lq, ls), ("pt", qx, sx)):
+            for b in range(4):
+                mm(V(out, 512 * b, 512 * b + C), V("eq", 128 * b, 128 * b + 128), V("es", 128 * b, 128 * b + 128), q, s)
+        later.append(lambda: diag("eo3", "bot", 256, C))
+        later.append(lambda: pickd(V("lb", 0, 14), "eo3", 0, C))
         if t == 0:
             order_constants()
-        gather2("ja", 32, V("bot"), "lps", 0, 16, 8)
-        src, dst = "ja", "jc"
-        for k in range(4):
-            diag("eo1", src, 48, 240, "sp%d" % k)
+        free = [("ja", 0), ("ja", 256), ("jc", 0), ("jc", 256)]
+
+        def table(x):
+            return V(x[0], x[1], x[1] + C)
+
+        def unpacked(k):
             act(V("tp", C * k, C * k + C), V("ph", 512 * k, 512 * k + C))
+
+        ta = free.pop(0)
+        gather2(ta[0], ta[1], V("bot"), "lps", 2, 16, 10)
+        act(V("ot", 1, 17), IND(V("bot"), V("lps", 0, 1)))
+        a, b, m, old, new = 1, 0, 2, 0, 16
+        for step in range(6):
+            co = (m + 15) // 16
+            tb = ta
+            if step < 5:
+                diag("eo1", ta[0], ta[1], C)
+            diag("eo2", "ot", 0, 16 * co)
+            if b:
+                tb = free.pop(0)
+                gather2(tb[0], tb[1], table(ta), "ld", old, old + 14, old + (6 if step == 5 else 0))
+            else:
+                unpacked(0)
+                unpacked(1)
+            if m < a + b:
+                act(V("ot", a, a + 16 * ((b + 15) // 16)), IND(table(ta), V("oq", old, old + (b + 15) // 16)))
             fill()
-            pickd(V("ol", 13, 28), "eo1", 0, 240)
-            fill()
-            gather2(dst, 32, V(src, 64, 512), "ol", 12, 28, 20)
-            src, dst = dst, src
-        diag("eo1", src, 48, 240)
-        pickd(V("ol", 13, 28), "eo1", 0, 240)
-        gather2(dst, 32, V(src, 64, 288), "ol", 12, 28, 20)
-        src, dst = dst, src
-        diag("eo1", src, 48, 240)
-        pickd(V("ol", 14, 28), "eo1", 16, 240)
-        pickd(V("ol", 12, 13), "eo1", 0, 16)
-        gather2(dst, 32, V(src, 64, 288), "ol", 12, 28, 20)
-        src, dst = dst, src
-        diag("eo1", src, 32, 256)
-        pickd(V("ol", 14, 28), "eo1", 32, 256)
-        pickd(V("ol", 10, 12), "eo1", 0, 32)
-        gather2(dst, 0, V(src, 64, 288), "ol", 10, 28, 18)
-        src, dst = dst, src
-        diag("eo1", src, 0, 64)
-        pickd(V("ol", 6, 10), "eo1", 0, 64)
-        gather2(dst, 64, V(src, 64, 288), "ol", 8, 14, 14)
-        diag("eo1", dst, 64, 96)
-        pickd(V("ol", 0, 6), "eo1", 0, 96)
-        send("l", t, V("ol", 0, 14), ll)
-        cp(IND(V("plr"), V("ol", 0, 14)), V("idp", 0, C))
+            if step < 5:
+                pickd(V("ld", new, new + 14), "eo1", 0, C)
+            pickd(V("oq", new, new + co), "eo2", 0, 16 * co)
+            if step < 5:
+                fill()
+                tc = free.pop(0)
+                gather2(tc[0], tc[1], table(tb), "ld", new, new + 14, new + 6)
+                cp(V("ot", a + b, a + b + 16 * co), IND(table(tb), V("oq", new, new + co)))
+                free.extend([ta] if tb == ta else [ta, tb])
+                ta = tc
+            else:
+                gather2("ot", a + b, table(tb), "oq", new, new + co, new + 2)
+            a, b, m, old, new = 2 * a + b, a, a + b + m, new, old
+        fill(9)
+        diag("eo2", "ot", 64, 64)
+        unpacked(2)
+        unpacked(3)
+        pickd(V("oq", 0, 4), "eo2", 0, 64)
+        cp(V("ot", 163, 227), IND(table(tb), V("oq", 0, 4)))
+        scan(V("eo1", 0, C), V("ot", 1, 225, -1), V("ex", 0, C), -1.0, A.max, A.add)
+        pickd(V("ol"), "eo1", 0, C)
+        send("l", t, V("ol"), ll)
+        cp(IND(V("plr"), V("ol")), V("idp", 0, C))
         act(V("rr"), IND(V("plr"), V("lb", 0, 14)))
         diag("eo1", "plr", 0, C)
         pickd(V("z", 56, 84, 2), "eo1", 0, C)
@@ -488,39 +489,40 @@ def rank_program(g, core, T, topo):
         pickd(V("z", 57, 84, 2), "eo2", 0, C)
         l, r, l4, i16, j16 = V("z", 56, 84, 2), V("z", 57, 84, 2), V("z", 28, 56, 2), V("z", 0, 28, 2), V("z", 1, 28, 2)
         w = [V("w1", 16 * k, 16 * k + 14) for k in range(8)]
+        nv = 2 if route(T, topo, rank, t)[0] != route(T, topo, rank, t)[1] else 1
         ts(V("z", 28, 56), V("z", 56, 84), 2, A.logical_shift_right)
         ts(V("z", 0, 28), V("z", 56, 84), 4, A.logical_shift_right)
-        ts(w[0], l4, 4.0, A.mult, float(XX - HH + 4), A.add)
         tt(V("dd", 0, 42), V("z", 1, 84, 2), V("z", 0, 84, 2), A.subtract)
+        ts(w[0], l4, 4.0, A.mult, float(XX - HH + 4), A.add)
         ts(w[1], j16, 1.0, A.add)
-        ts(w[3], V("dd", 14, 28), -1.0, A.add, 0.0, A.max)
         ts(w[2], i16, -2.0, A.mult, float(YY - HH - 2), A.add)
-        tt(V("dd", 14, 28), V("dd", 14, 28), V("dd", 0, 14), A.add)
+        ts(w[3], V("dd", 14, 28), -1.0, A.add, 0.0, A.max)
+        tt(V("ff", 28, 42), V("dd", 14, 28), V("dd", 0, 14), A.add)
+        ts(V("ff", 14, 28), V("dd", 28, 42), 3.0, A.is_ge)
         ts(w[4], V("dd", 28, 42), 1.0, A.min)
-        tt(V("ff", 0, 28), V("dd", 14, 42), V("th", 0, 28), A.is_ge)
         tt(w[1], w[1], j16, A.mult)
-        tt(w[5], V("ff", 0, 14), V("ff", 14, 28), A.add)
-        nv = 2 if route(T, topo, rank, t)[0] != route(T, topo, rank, t)[1] else 1
+        ts(V("ff", 0, 14), V("ff", 28, 42), 4.0, A.is_ge)
         for b in range(nv, 4):
             act(V("bt", b, D, 4), IND(V("tp", C * b, C * b + C), ll))
         for b in range(nv):
             cp(V("bt", b, D, 4), IND(V("tp", C * b, C * b + C), ll))
+        tt(w[5], V("ff", 0, 14), V("ff", 14, 28), A.add)
+        tt(V("mm", 14, 28), w[0], w[3], A.add)
+        tt(V("mm", 0, 14), w[1], w[2], A.add)
         quant(V("fq"), V("fs"), V("bt"))
         for b in range(4):
             mm(V("ph", 512 * b, 512 * b + C), V("wq", 128 * b, 128 * b + 128), V("wp", 128 * b, 128 * b + 128), V("fq"), V("fs"))
         for b in range(4):
             act(V("tab", HH + C * b, HH + C * b + C), V("ph", 512 * b, 512 * b + C), AF.Copy, 0.03125)
         ts(w[5], w[5], float(D), A.mult)
-        tt(V("mm", 14, 28), w[0], w[3], A.add)
-        tt(V("mm", 0, 14), w[1], w[2], A.add)
+        tt(V("dd", 0, 28), V("ff", 0, 28), V("mm", 0, 28), A.mult)
         tt(w[4], w[4], l, A.add)
         tt(w[6], l, w[5], A.add)
         tt(w[7], r, w[5], A.subtract)
-        tt(V("dd", 0, 28), V("ff", 0, 28), V("mm", 0, 28), A.mult)
+        tt(w[3], V("dd", 0, 14), V("dd", 14, 28), A.max)
         cp(V("lr", 0, 14), w[6])
-        tt(w[4], w[4], V("dd", 0, 14), A.max)
         ts(V("lr", 16, 30), w[7], float(HH), A.add)
-        tt(w[4], w[4], V("dd", 14, 28), A.max)
+        tt(w[4], w[4], w[3], A.max)
         for b in range(4):
             scan(V("tab", S16 + C * b, S16 + C * b + C, -1), V("k16", 0, C), V("tab", HH + C * b, HH + C * b + C, -1), 0.0, A.add, A.max)
             if b == 0:

@@ -2,11 +2,24 @@ from concourse.mybir import dt, AluOpType, AxisListType, ActivationFunctionType
 
 C, R = 224, 3
 D = 4 * C
+HA = 128
 TRI = 1680
 BIG = 1.0e29
 MAGIC = 12582912.0
 P16, P4, HH, S4, S16, XX, YY = [k * D for k in range(7)]
 TABW = 7 * D + 32
+SLOTS = 8
+
+CYCLE, WAKE, LOCAL, REMOTE = 0.87, 200.0, 2000.0, 1600.0
+TURNS, STRETCH = 900, 6000.0
+PSV = range(14)
+WHOLE = ((P16, P4, S4), (P4, P16))
+B1, B2, M1, M2 = 0, 0, 8, 8
+SEQ = "aa"
+BV = (((2, 3), ()), ((2, 3), (3,)))
+NB = 2
+LCV = 5
+PSS = ((0, 5), (5, 7), (7, 9), (9, 10), (10, 11), (11, 12), (12, 13), (13, 14))
 
 BF, F32, I32, U16, X4, U8 = "bfloat16", "float32", "int32", "uint16", "float8_e4m3fn_x4", "uint8"
 SCRATCH = {}
@@ -19,19 +32,19 @@ def _sb(name, n, t):
 for _n, _w, _t in [
     ("xt", D, BF), ("xs", D, BF), ("ut", 512, BF), ("vt", 512, BF), ("ez", 528, BF), ("eo", 528, BF),
     ("eq", 512, X4), ("es", 512, U8), ("uq", 128, X4), ("us", 128, U8), ("vq", 128, X4), ("vs", 128, U8),
-    ("wq", 512, X4), ("wp", 512, U8), ("fq", C, X4), ("fs", C, U8), ("tp", D, BF), ("bt", D, BF),
+    ("wq", 512, X4), ("wp", 512, U8), ("fq", 256, X4), ("fs", 256, U8), ("tp", D, BF), ("bt", 1024, BF),
     ("idp", 272, BF), ("lx", 16, U16), ("px", 48, BF), ("ci", 16, I32), ("cf", 16, F32), ("cg", 16, F32), ("cl", 8, U16),
-    ("wtb", 16, F32), ("wtm", 16, F32), ("thr", 2, F32), ("jb", 32, F32), ("d0", 480, BF),
-    ("zf", 256, BF), ("tt", 480, BF), ("to", 480, BF), ("pl16", 16, U16), ("pwb", 16, BF), ("pwf", 16, F32),
+    ("wtb", 16, F32), ("wtm", 16, F32), ("wtn", 16, F32), ("thr", 2, F32), ("jb", 32, F32), ("d0", C, BF), ("rm", C, BF),
+    ("zf", C, BF), ("tt", C, BF), ("to", C, BF), ("tr", C, BF), ("pwf", 16, F32),
     ("prep", C, BF), ("pout", C, F32), ("ccb", 16, BF), ("ccn", 16, F32), ("pat", 16, BF), ("pbk", 16, BF), ("pb2", 16, BF),
     ("klc", TRI, BF), ("kps", TRI, BF), ("xlc", TRI, BF), ("xps", TRI, BF), ("olc", TRI, BF), ("ops", TRI, BF),
-    ("ex", 256, BF), ("eo1", 256, BF), ("eo2", 256, BF), ("eo3", 256, BF),
-    ("ld", 32, U16), ("lps", 16, U16), ("pt1", 16, F32), ("pt2", 16, F32),
-    ("ja", 512, BF), ("jc", 512, BF), ("bot", 480, BF), ("ol", 14, U16), ("oq", 32, U16), ("ot", 240, BF),
-    ("lb", 16, U16), ("plr", C, BF), ("rr", C, BF),
-    ("z", 96, I32), ("dd", 48, I32), ("ff", 48, I32), ("th", 48, I32), ("mm", 48, I32), ("w1", 128, I32), ("lr", 48, U16),
+    ("ex", 256, BF), ("eb", SLOTS * C, BF), ("jt", SLOTS * C, BF), ("ld", SLOTS * 16, U16),
+    ("lps", 16, U16), ("pt1", 16, F32), ("pt2", 16, F32),
+    ("bot", 480, BF), ("om", (C - HA) // 16, U16), ("ol", HA // 16, U16), ("ot", 240, BF), ("lb", 16, U16), ("plr", C, BF), ("rr", C, BF),
+    ("z", 96, I32), ("dd", 48, I32), ("de", 32, I32), ("ff", 48, I32), ("mm", 48, I32), ("w1", 192, I32), ("lr", 48, U16),
     ("tab", TABW, F32), ("k4", D, F32), ("k16", D, F32), ("sq", 96, BF), ("ksq", 96, F32), ("lsq", 24, U16),
     ("mseq", 384, F32), ("ga", D, F32), ("gb", D, F32), ("gm", D, F32), ("yo", C, F32),
+    ("k3", 3 * C, F32), ("g3", 3 * D, F32), ("o3", 3 * D, F32), ("ja", C, BF), ("pwn", 16, F32),
 ]:
     _sb(_n, _w, _t)
 for _k in range(R + 1):
@@ -40,12 +53,13 @@ for _k in range(R + 1):
 for _k in range(R):
     _sb("lq%d" % _k, C, X4)
     _sb("ls%d" % _k, C, U8)
-    _sb("ll%d" % _k, 14, U16)
+    _sb("lm%d" % _k, (C - HA) // 16, U16)
+    _sb("ll%d" % _k, HA // 16, U16)
 SCRATCH["pt"] = ("psum", [128, 2048], F32)
 SCRATCH["ph"] = ("psum", [128, 2048], F32)
 
 SEMAPHORES = ["ev", "ea", "et", "eg"] + ["dm%d" % k for k in range(16)] + \
-    [a + b + str(k) for a in "as" for b in "qsl" for k in range(R)]
+    [a + b + str(k) for a in "as" for b in "qsml" for k in range(R)]
 
 
 def count(mask):
@@ -69,11 +83,78 @@ def hand_on(g, core, T, topo):
             n_in = count(topo.mask(T.cores[r], core))
             rid, pid = topo.addr(dst, core)
             m = topo.mask(core, dst)
-            for k, ap in (("q", T["lq%d" % t][:].bitcast(dt.uint8)), ("s", T["ls%d" % t][:]), ("l", T["ll%d" % t][:])):
+            for k in "qsml":
+                ap = T["l%s%d" % (k, t)][:]
+                if k == "q":
+                    ap = ap.bitcast(dt.uint8)
                 g.wait_ge(T.sem["a%s%d" % (k, t)], n_in)
                 g.remote_dma(ap, ap, T.sem["a%s%d" % (k, t)], T.sem["s%s%d" % (k, t)], pid, rid, m)
-            for k in "qsl":
+            for k in "qsml":
                 g.wait_ge(T.sem["s%s%d" % (k, t)], count(m))
+
+
+def lay(calls, order, before):
+    start, busy = [0.0] * len(calls), {}
+    for k in order:
+        queue, time, hold = calls[k]
+        at = 0.0
+        for j in before[k]:
+            at = max(at, start[j] + calls[j][1] + WAKE)
+        if queue:
+            taken = busy.setdefault(queue, [])
+            i = len(taken)
+            while i and taken[i - 1][1] > at:
+                i -= 1
+            while i < len(taken) and at + hold > taken[i][0]:
+                at = max(at, taken[i][1])
+                i += 1
+            taken.insert(i, (at, at + hold))
+        start[k] = at
+    return start
+
+
+PLACED = {}
+
+
+def place(calls):
+    key = tuple((c["queue"], c["time"], c["hold"]) for c in calls)
+    if key in PLACED:
+        return PLACED[key]
+    n = len(calls)
+    before = [sorted(c["after"]) for c in calls]
+    behind = [[] for c in calls]
+    chain = [c["time"] for c in calls]
+    for k in range(n - 1, -1, -1):
+        for j in before[k]:
+            behind[j].append(k)
+            chain[j] = max(chain[j], key[j][1] + WAKE + chain[k])
+
+    def tighten(rank, turns):
+        best = None
+        for turn in range(turns):
+            start = lay(key, sorted(range(n), key=lambda k: (rank[k], k)), before)
+            end = max(start[k] + key[k][1] for k in range(n))
+            if best is None or end < best[0]:
+                best = (end, start)
+            if turn + 1 < turns:
+                back = lay(key, sorted(range(n), key=lambda k: (-start[k] - key[k][1], -k)), behind)
+                rank = [-back[k] - key[k][1] for k in range(n)]
+        return best
+
+    best = tighten([-c for c in chain], 4)
+    mix = 1
+    for turn in range(TURNS):
+        first, width = turn * 0.618034 % 1 * best[0], (450.0, 1200.0, 3000.0)[turn % 3]
+        rank = list(best[1])
+        for k in range(n):
+            if first < rank[k] < first + STRETCH:
+                mix = mix * 16807 % 2147483647
+                rank[k] += width * (mix / 2147483647 - 0.5)
+            for j in before[k]:
+                rank[k] = max(rank[k], rank[j])
+        best = min(tighten(rank, 2), best, key=lambda x: x[0])
+    PLACED[key] = sorted(range(n), key=lambda k: (best[1][k], k))
+    return PLACED[key]
 
 
 def rank_program(g, core, T, topo):
@@ -84,12 +165,9 @@ def rank_program(g, core, T, topo):
     A = AluOpType
     AF = ActivationFunctionType
     Q = {"v": g.vector, "a": g.scalar, "t": g.tensor, "g": g, "s": g.sync}
-    cnt = {"ev": 0, "ea": 0, "et": 0, "eg": 0}
-    known = {e: {} for e in Q}
-    clock = {}
+    calls = []
     recs = {}
-    totals = {}
-    ndma = [0]
+    turns = {"eb": 0, "jt": 0, "ld": 0, "dm": 0}
 
     def V(name, a=0, b=None, s=1):
         w = SCRATCH[name][1][1]
@@ -107,24 +185,19 @@ def rank_program(g, core, T, topo):
             ap = T[name][:, a:b]
         else:
             ap = T[name][:, a:b:s]
-        return (ap, name, m, [])
+        return (ap, name, m, [], len(range(a, b, abs(s))))
 
     def IND(win, off):
-        return (win[0].indirect(off[0]), win[1], win[2], [off])
+        return (win[0].indirect(off[0]), win[1], win[2], [off], 16 * off[4])
 
     def ap(x):
         return x[0] if isinstance(x, tuple) else x
 
-    def need(e, ev):
-        s, n = ev
-        if known[e].get(s, 0) >= n:
-            return
-        Q[e].wait_ge(T.sem[s], n)
-        for s2, n2 in clock[ev].items():
-            if known[e].get(s2, 0) < n2:
-                known[e][s2] = n2
+    def slot(name, width):
+        turns[name] += 1
+        return turns[name] % SLOTS * width
 
-    def order(e, writes, reads):
+    def add(queue, writes, reads, call, time, hold=None, sem=None, more=()):
         rd = []
         for x in reads:
             if isinstance(x, tuple):
@@ -134,174 +207,156 @@ def rank_program(g, core, T, topo):
             rd.extend(x[3])
         wr = list(writes) + [x for x in rd if SCRATCH[x[1]][0] == "psum"]
         rd = [x for x in rd if SCRATCH[x[1]][0] != "psum"]
-        evs = {}
+        after = set(more)
         for x in wr:
-            for m, ev, w in recs.get(x[1], []):
-                if m & x[2]:
-                    evs[ev[0]] = max(evs.get(ev[0], 0), ev[1])
+            after.update(k for m, k, w in recs.get(x[1], []) if m & x[2])
         for x in rd:
-            for m, ev, w in recs.get(x[1], []):
-                if w and m & x[2]:
-                    evs[ev[0]] = max(evs.get(ev[0], 0), ev[1])
-        for s in sorted(evs, key=lambda s: s == "e" + e):
-            need(e, (s, evs[s]))
-        return wr, rd
-
-    def note(e, ev, wr, rd):
-        clock[ev] = dict(known[e])
-        clock[ev][ev[0]] = ev[1]
-        totals[ev[0]] = ev[1]
+            after.update(k for m, k, w in recs.get(x[1], []) if w and m & x[2])
+        k = len(calls)
+        calls.append({"queue": queue, "call": call, "time": time, "hold": time if hold is None else hold, "sem": sem, "after": after})
         for x in wr:
-            recs[x[1]] = [(m & ~x[2], v, w) for m, v, w in recs.get(x[1], []) if m & ~x[2]] + [(x[2], ev, True)]
+            recs[x[1]] = [(m & ~x[2], v, w) for m, v, w in recs.get(x[1], []) if m & ~x[2]] + [(x[2], k, True)]
         for x in rd:
-            recs.setdefault(x[1], []).append((x[2], ev, False))
+            recs.setdefault(x[1], []).append((x[2], k, False))
+        return k
 
-    def op(e, writes, reads, call):
-        wr, rd = order(e, writes, reads)
-        s = "e" + e
-        cnt[s] += 1
-        call().then_inc(T.sem[s], 1)
-        note(e, (s, cnt[s]), wr, rd)
+    def op(e, out, reads, call, cycles=1.0):
+        full = [x for x in [out] + reads if isinstance(x, tuple) and x[4] > 1]
+        if out[3]:
+            time = (60 + 3.8 * out[4]) * CYCLE
+        elif reads and reads[0][3]:
+            time = ((60 if e == "v" else 78) + 1.56 * out[4]) * CYCLE
+        else:
+            if e == "v" and all(SCRATCH[x[1]][2] in (BF, U16) for x in full):
+                cycles /= 2
+            time = (max(64, cycles * (reads[0] if reads else out)[4]) + 26) * CYCLE
+        add(e, [out], reads, call, time)
 
     def dma(e, out, in_, writes, reads):
-        wr, rd = order(e, writes, reads)
-        s = "dm%d" % ndma[0]
-        ndma[0] += 1
-        Q[e].dma_start(out, in_).then_inc(T.sem[s], 16)
-        note(e, (s, 16), wr, rd)
+        turns["dm"] += 1
+        add(e, writes, reads, lambda: Q[e].dma_start(out, in_), LOCAL, 100.0, ("dm%d" % turns["dm"], 16))
 
     def send(kind, t, src, land):
         hop, dst = route(T, topo, rank, t)
-        wr, rd = order("g", [], [src])
         rid, pid = topo.addr(hop, core)
         m = topo.mask(core, hop)
         a, b = src[0], land[0]
         if kind == "q":
             a, b = a.bitcast(dt.uint8), b.bitcast(dt.uint8)
-        g.remote_dma(b, a, T.sem["a%s%d" % (kind, t)], T.sem["s%s%d" % (kind, t)], pid, rid, m)
-        note("g", ("s%s%d" % (kind, t), count(m)), wr, rd)
+        arrive, leave = "a%s%d" % (kind, t), "s%s%d" % (kind, t)
+        time = REMOTE * (1 if kind in "ml" else 4)
+        k = add("g", [], [src], lambda: g.remote_dma(b, a, T.sem[arrive], T.sem[leave], pid, rid, m), time, 100.0, (leave, count(m)))
         hop2, me = route(T, topo, rank ^ (1 << t), t)
         last = dst if hop2 == me else hop2
-        ev = ("a%s%d" % (kind, t), count(topo.mask(last, core)))
-        clock[ev] = {ev[0]: ev[1]}
-        totals[ev[0]] = ev[1]
-        recs[land[1]] = [(land[2], ev, True)]
+        add(None, [land], [], None, 1.0 if hop == dst else time, 0.0, (arrive, count(topo.mask(last, core))), [k])
 
     def ts(out, in0, s1, o0, s2=None, o1=None):
         if o1 is None:
-            op("v", [out], [in0, s1], lambda: g.vector.tensor_scalar(out[0], in0[0], ap(s1), None, o0))
+            op("v", out, [in0, s1], lambda: g.vector.tensor_scalar(out[0], in0[0], ap(s1), None, o0))
         else:
-            op("v", [out], [in0, s1, s2], lambda: g.vector.tensor_scalar(out[0], in0[0], ap(s1), ap(s2), o0, o1))
+            op("v", out, [in0, s1, s2], lambda: g.vector.tensor_scalar(out[0], in0[0], ap(s1), ap(s2), o0, o1))
 
     def tt(out, a, b, o):
-        op("v", [out], [a, b], lambda: g.vector.tensor_tensor(out[0], a[0], b[0], o))
+        op("v", out, [a, b], lambda: g.vector.tensor_tensor(out[0], a[0], b[0], o), 1.0 if SCRATCH[b[1]][0] == "psum" else 2.0)
 
     def cp(out, a):
-        op("v", [out], [a], lambda: g.vector.tensor_copy(out[0], a[0]))
+        op("v", out, [a], lambda: g.vector.tensor_copy(out[0], a[0]))
 
     def ms(out, c):
-        op("v", [out], [], lambda: g.vector.memset(out[0], c))
+        op("v", out, [], lambda: g.vector.memset(out[0], c))
 
     def scan(out, d0, d1, init, o0, o1):
-        op("v", [out], [d0, d1], lambda: g.vector.tensor_tensor_scan(out[0], d0[0], d1[0], init, o0, o1))
+        op("v", out, [d0, d1], lambda: g.vector.tensor_tensor_scan(out[0], d0[0], d1[0], init, o0, o1))
+
+    def turn(out, a):
+        op("v", out, [a], lambda: g.vector.transpose(out[0], a[0]))
 
     def act(out, a, f=AF.Copy, scale=1.0, bias=None):
         if bias is None:
-            op("a", [out], [a], lambda: g.scalar.activation(out[0], a[0], f, scale=scale))
+            op("a", out, [a], lambda: g.scalar.activation(out[0], a[0], f, scale=scale))
         else:
-            op("a", [out], [a, bias], lambda: g.scalar.activation(out[0], a[0], f, bias=ap(bias), scale=scale))
+            op("a", out, [a, bias], lambda: g.scalar.activation(out[0], a[0], f, bias=ap(bias), scale=scale))
 
     def quant(q, s, x):
-        op("v", [q, s], [x], lambda: g.vector.quantize_mx(q[0], s[0], x[0]))
+        add("v", [q, s], [x], lambda: g.vector.quantize_mx(q[0], s[0], x[0]), (14 + 0.265 * x[4]) * CYCLE)
 
     def mm(out, lq, ls, rq, rs):
-        op("t", [out], [lq, ls, rq, rs], lambda: g.tensor.matmul_mx(out[0], lq[0], ls[0], rq[0], rs[0], True, True))
+        add("t", [out], [lq, ls, rq, rs], lambda: g.tensor.matmul_mx(out[0], lq[0], ls[0], rq[0], rs[0], True, True), 40 + 0.6 * rq[4])
 
     def iota(out, pat, base=0, cm=0):
         if SCRATCH[out[1]][2] == I32:
-            op("g", [out], [], lambda: g.iota(out[0], pat, base, cm))
+            add("g", [out], [], lambda: g.iota(out[0], pat, base, cm), (157 + 2 * out[4]) * CYCLE)
         else:
-            op("g", [out], [], lambda: g.iota(out[0], pat, base, cm, allow_small_or_imprecise_dtypes=True))
+            add("g", [out], [], lambda: g.iota(out[0], pat, base, cm, allow_small_or_imprecise_dtypes=True), (157 + 2 * out[4]) * CYCLE)
 
     def asel(out, a, pat, cmp, fill_, base, cm):
-        op("g", [out], [a], lambda: g.affine_select(out[0], a[0], pat, cmp, fill_, base, cm))
+        add("g", [out], [a], lambda: g.affine_select(out[0], a[0], pat, cmp, fill_, base, cm), (205 + 2 * out[4]) * CYCLE)
 
-    def gather2(out, o0, win, off, c0, c1, cv):
-        if cv < c1:
-            act(V(out, o0 + 16 * (cv - c0), o0 + 16 * (c1 - c0)), IND(win, V(off, cv, c1)))
-        if cv > c0:
-            cp(V(out, o0, o0 + 16 * (cv - c0)), IND(win, V(off, c0, cv)))
+    def gather2(out, o0, win, off, c0, cv, n=14):
+        if cv < n:
+            act(V(out, o0 + 16 * cv, o0 + 16 * n), IND(win, V(off, c0 + cv, c0 + n)))
+        if cv > 0:
+            cp(V(out, o0, o0 + 16 * cv), IND(win, V(off, c0, c0 + cv)))
 
-    def diag(eo, src, a, n):
-        scan(V(eo, 0, n), V(src, a, a + n), V("ex", 0, n), -1.0, A.max, A.add)
+    def listed(out, src, *more):
+        a = slot("eb", C)
+        scan(V("eb", a, a + src[4]), src, V("ex", 0, src[4]), -1.0, A.max, A.add)
+        ts(out, V("eb", a + 15, a + src[4], 16), 256.0, A.add, *more)
 
-    def pickd(out, eo, a, n):
-        ts(out, V(eo, a + 15, n, 16), 256.0, A.add)
+    def table(a):
+        return V("jt", a, a + C)
 
-    def scores(t):
-        qx, sx = V("qx%d" % t), V("sx%d" % t)
-        quant(qx, sx, V("xt" if t == 0 else "xs"))
-        mm(V("ph", 0, C), V("uq"), V("us"), qx, sx)
+    def power(win, lst, cv):
+        a = slot("jt", C)
+        gather2("jt", a, win, "ld", lst, cv)
+        return a
 
-    later = []
-
-    def fill(n=1):
-        for k in range(min(n, len(later))):
-            later.pop(0)()
+    def new_list(src):
+        a = slot("ld", 16)
+        listed(V("ld", a, a + src[4] // 16), src)
+        return a
 
     dma("s", T.xt[:], T.x[:], [V("xt")], [])
     dma("a", T.ut[:], T.u[:], [V("ut")], [])
     dma("s", T.wq[:].bitcast(dt.uint8), T.wc[:], [V("wq")], [])
     dma("s", T.wp[:], T.ws[:], [V("wp")], [])
     dma("s", T.vt[:], T.v[:], [V("vt")], [])
+    quant(V("uq"), V("us"), V("ut"))
+    quant(V("vq"), V("vs"), V("vt"))
 
     iota(V("ci", 0, 1), [[0, 1]], 0, 1)
     iota(V("idp"), [[1, 272]])
     iota(V("jb", 0, 14), [[32, 7], [0, 2]])
-    iota(V("jb", 14, 30), [[32, 8], [0, 2]], -16)
-    iota(V("kps"), [[0, TRI]], -1)
-    p = V("ci", 0, 1)
-    ms(V("d0"), 0.5)
-    ms(V("zf"), 0.0)
-    ts(V("ci", 1, 2), p, 15, A.bitwise_and)
-    ts(V("ci", 2, 3), p, 31, A.bitwise_and)
-    ts(V("ci", 3, 4), p, 4, A.logical_shift_right)
-    ms(V("wtb", 0, 8), 128.0)
-    ms(V("wtb", 8, 9), -127.5 / 256)
-    ms(V("wtb", 9, 10), MAGIC)
-    tt(V("ci", 4, 5), p, V("ci", 3, 4), A.add)
-    ms(V("wtb", 10, 11), -MAGIC)
-    ms(V("wtb", 11, 13), 256.0)
-    ms(V("wtb", 13, 16), 0.0)
-    ts(V("ci", 5, 6), V("ci", 4, 5), 1, A.bitwise_and)
-    ms(V("d0", 0, 480, 16), 0.0)
-    ms(V("d0", 9, 480, 16), 1.0)
-    ms(V("d0", 10, 480, 16), 1.0)
-    cp(V("cf", 0, 6), V("ci", 0, 6))
-    ms(V("d0", 11, 480, 16), -1.0)
-    pm16, pm32, par = V("cf", 1, 2), V("cf", 2, 3), V("cf", 5, 6)
-    ts(V("pat"), V("idp", 0, 16), pm16, A.max)
+    ts(V("ci", 1, 2), V("ci", 0, 1), 15, A.bitwise_and)
+    ts(V("ci", 2, 3), V("ci", 0, 1), 31, A.bitwise_and)
+    cp(V("cf", 1, 3), V("ci", 1, 3))
+    pm16, pm32 = V("cf", 1, 2), V("cf", 2, 3)
+    for a, b, c in ((0, 8, -128.0), (8, 11, 0.0), (11, 12, 127.5 / 256), (12, 14, -MAGIC), (14, 15, 1.0), (15, 16, 0.0)):
+        ms(V("wtb", a, b), c)
     ts(V("wtm"), V("idp", 0, 16), pm16, A.is_equal)
-    ts(V("pb2"), V("idp", 0, 16), pm16, A.add, 15.5, A.is_le)
+    tt(V("wtn"), V("wtm"), V("wtb"), A.mult)
+    op("v", V("thr", 1, 2), [V("wtn")], lambda: g.vector.tensor_reduce(T.thr[:, 1:2], T.wtn[:], AxisListType.X, A.add))
     ts(V("thr", 0, 1), pm16, 7.5, A.is_gt, -BIG, A.mult)
-    ts(V("d0", 8, 480, 16), V("jb", 0, 30), pm32, A.add, 1.0 / 256, A.mult)
-    tt(V("wtm"), V("wtm"), V("wtb"), A.mult)
+    ms(V("d0"), 0.5)
+    for k, c in ((0, 0.0), (12, 1.0), (13, -1.0), (14, 1.0)):
+        ms(V("d0", k, C, 16), c)
+    ts(V("d0", 11, C, 16), V("jb", 0, 14), pm32, A.add, 1.0 / 32, A.mult)
+    ts(V("jb", 16, 30), V("d0", 11, C, 16), 0.0, A.is_equal, 255.0, A.mult)
+    ts(V("d0", 15, C, 16), V("jb", 16, 30), 1.0, A.add)
+    ms(V("rm"), 1.0)
+    ms(V("rm", 15, C, 16), 0.0)
+    iota(V("kps"), [[0, TRI]], -1)
+    ts(V("pat"), V("idp", 0, 16), pm16, A.max)
+    ts(V("pb2"), V("idp", 0, 16), pm16, A.add, 15.5, A.is_le)
     ts(V("pbk"), V("pb2"), 1025.0, A.mult, -1.0, A.add)
-    ts(V("cg", 0, 1), pm16, 16.0, A.mult, 12.0, A.add)
-    ts(V("cg", 1, 2), pm16, -1.0, A.mult, 14.0, A.add)
-    op("v", [V("thr", 1, 2)], [V("wtm")], lambda: g.vector.tensor_reduce(T.thr[:, 1:2], T.wtm[:], AxisListType.X, A.add))
-    quant(V("uq"), V("us"), V("ut"))
-    scores(0)
-    ts(V("cg", 2, 3), pm16, 1.0, A.add, 14.0, A.min)
-    ts(V("ccb", 0, 14), V("idp", 0, C, 16), pm16, A.add)
-    ts(V("cg", 1, 2), V("cg", 1, 2), 1.0, A.max)
-    ts(V("d0", 12, 480, 16), V("d0", 8, 480, 16), 0.0, A.not_equal, -1.0, A.mult)
-    ts(V("cg", 3, 4), par, 240.0, A.mult, V("cg", 0, 1), A.add)
+    ts(V("ccb", 0, 14), V("idp", 1, C, 16), pm16, A.add)
     ts(V("ccn", 0, 14), V("ccb", 0, 14), -512.0, A.mult)
+    ts(V("cg", 0, 1), pm16, -1.0, A.mult, 14.0, A.add)
+    ts(V("cg", 1, 2), V("cg", 0, 1), 1.0, A.max)
+    ts(V("cg", 2, 3), pm16, 1.0, A.add, 14.0, A.min)
     ts(V("cg", 4, 6), V("cg", 1, 3), 1.0, A.add, 8.0, A.mult)
-    ts(V("px", 0, 16), V("idp", 0, 16), pm16, A.is_equal, 256.0, A.mult)
-    ts(V("cl", 0, 1), V("cg", 3, 4), 476.0, A.min)
-    ts(V("px", 16, 32), V("idp", 0, 16), pm16, A.is_lt, -256.0, A.mult)
+    tt(V("cg", 6, 8), V("cg", 4, 6), V("cg", 1, 3), A.mult)
+    ts(V("cl", 2, 6, 2), V("cg", 6, 8), -1.0, A.add)
 
     def seg_lc(m):
         n = 14 - m
@@ -315,244 +370,228 @@ def rank_program(g, core, T, topo):
         a, n = seg_lc(m)
         if n > 16:
             act(V("klc", a + 16, a + n), V("idp", 16 * m + 16, C), AF.Identity, -1.0, 256.0)
-    for m in range(14):
-        a, n = seg_lc(m)
         act(V("klc", a, a + 16), V("pat"), AF.Identity, -1.0, 256.0 - 16 * m)
-    for m in range(14):
         a, n = seg_ps(m)
         act(V("kps", a, a + 16), V("pbk"))
-
-    def late_vector_constants():
-        later.extend([
-            lambda: tt(V("px", 32, 48), V("px", 0, 16), V("px", 16, 32), A.add),
-            lambda: tt(V("cg", 6, 8), V("cg", 4, 6), V("cg", 1, 3), A.mult),
-            lambda: ts(V("px", 47, 48), V("px", 47, 48), -512.0, A.add),
-            lambda: ts(V("lx"), V("idp", 0, 16), 0.0, A.mult, pm16, A.add),
-            lambda: ts(V("cl", 2, 6, 2), V("cg", 6, 8), -1.0, A.add),
-            lambda: ms(V("lps", 0, 2), 256)])
-
-    def jump_constants():
-        for b in range(4):
-            later.append(lambda b=b: quant(V("eq", 128 * b, 128 * b + 128), V("es", 128 * b, 128 * b + 128), V("ez", 3 - b, 515 - b)))
-        later.append(lambda: ms(V("ot"), 0.0))
-
-    def order_constants():
-        later.append(lambda: ts(V("ksq"), V("sq"), D / 16, A.is_equal, -BIG, A.mult))
-        later.append(lambda: diag("eo3", "sq", 0, 96))
-        for b in range(4):
-            later.append(lambda b=b: ts(V("lsq", 6 * b, 6 * b + 6), V("eo3", 15, 96, 16), 16.0, A.mult, 4096.0 + C * b, A.add))
-
-    def late_constants():
-        iota(V("eo"), [[0, 528]], 1)
-        asel(V("ez"), V("eo"), [[1, 528]], A.is_equal, 0.0, -3, -4)
-        iota(V("bot", 0, 256), [[1, 256]])
-        iota(V("th", 0, 28), [[-1, 2], [0, 14]], 4)
-        iota(V("pout", 0, 1), [[0, 1]])
-        iota(V("sq"), [[0, 96]], D // 16)
-        for j in range(2, 14):
-            a = j * (j - 1) // 2 + 1
-            iota(V("sq", a, a + j - 1), [[-1, j - 1]], j - 1)
-        iota(V("tab", YY, TABW), [[0, D + 32]])
-        asel(V("k16"), V("tab", YY, YY + D), [[0, D // 16], [1, 16]], A.is_gt, -BIG, 0, 0)
-        asel(V("tab", XX, YY), V("k16"), [[0, D]], A.is_gt, -BIG, 0, 0)
-        asel(V("k4"), V("k16"), [[0, C], [1, 4]], A.is_gt, -BIG, 0, 0)
+    ts(V("px", 0, 16), V("idp", 0, 16), pm16, A.is_equal, 256.0, A.mult)
+    ts(V("px", 16, 32), V("idp", 0, 16), pm16, A.is_lt, -256.0, A.mult)
+    tt(V("px", 32, 48), V("px", 0, 16), V("px", 16, 32), A.add)
+    ts(V("px", 47, 48), V("px", 47, 48), -512.0, A.add)
+    ts(V("lx"), V("idp", 0, 16), 0.0, A.mult, pm16, A.add)
+    act(V("ex"), IND(V("px", 32, 48), V("lx")))
+    ms(V("ot"), 0.0)
+    ms(V("bt", 4 * (C - HA), 512), 0.0)
+    iota(V("bot", 0, 256), [[1, 256]], -1)
+    iota(V("pout", 0, 1), [[0, 1]])
+    iota(V("eo"), [[0, 528]], 1)
+    asel(V("ez"), V("eo"), [[1, 528]], A.is_equal, 0.0, -3, -4)
+    for b in range(4):
+        quant(V("eq", 128 * b, 128 * b + 128), V("es", 128 * b, 128 * b + 128), V("ez", 3 - b, 515 - b))
+    iota(V("sq"), [[0, 96]], D // 16)
+    for j in range(2, 14):
+        a = j * (j - 1) // 2 + 1
+        act(V("sq", a, a + j - 1), V("idp", 1, j, -1))
+    iota(V("tab", YY, TABW), [[0, D + 32]])
+    asel(V("tab", XX, YY), V("tab", YY, YY + D), [[0, D]], A.is_gt, -BIG, 0, 0)
+    for name, n in (("k16", 16), ("k4", 4), ("k3", 3)):
+        w = SCRATCH[name][1][1]
+        asel(V(name), V("tab", YY, YY + w), [[0, w // n], [1, n]], A.is_gt, -BIG, 0, 0)
+    ts(V("ksq"), V("sq"), D / 16, A.is_equal, -BIG, A.mult)
+    listed(V("pt1", 0, 6), V("sq"), 16.0, A.mult)
+    for b in range(4):
+        ts(V("lsq", 6 * b, 6 * b + 6), V("pt1", 0, 6), float(C * b), A.add, float(D), A.min)
 
     for t in range(R):
         qx, sx = V("qx%d" % t), V("sx%d" % t)
-        lq, ls, ll = V("lq%d" % t), V("ls%d" % t), V("ll%d" % t)
-        if t:
-            scores(t)
+        lq, ls, lm, ll = [V("l%s%d" % (k, t)) for k in "qsml"]
+        quant(qx, sx, V("xt" if t == 0 else "xs"))
+        mm(V("ph", 0, C), V("uq"), V("us"), qx, sx)
         send("q", t, qx, lq)
         send("s", t, sx, ls)
-        if t == 0:
-            late_constants()
-            late_vector_constants()
-        ts(V("zf", 16, 240), V("ph", 0, C), V("thr", 0, 1), A.is_gt, V("thr", 1, 2), A.mult)
-        fill()
-        op("v", [V("tt", 0, C)], [V("zf")], lambda: g.vector.transpose(T.tt[:, 0:C], T.zf[:, 16:240]))
-        op("v", [V("tt", C, 480)], [V("zf")], lambda: g.vector.transpose(T.tt[:, C:480], T.zf[:]))
-        fill()
+        ts(V("zf"), V("ph", 0, C), V("thr", 0, 1), A.is_gt, V("thr", 1, 2), A.mult)
+        turn(V("tt"), V("zf"))
         scan(V("to"), V("d0"), V("tt"), 0.0, A.mult, A.add)
-        fill()
-        cp(V("pl16"), IND(V("to"), V("cl", 0, 1)))
-        fill()
-        gather2("prep", 0, V("idp"), "pl16", 0, 14, 8)
-        fill(9)
-        for m in range(13, 4, -1):
+        scan(V("tr", 0, C, -1), V("rm", 0, C, -1), V("to", 0, C, -1), 0.0, A.mult, A.max)
+        turn(V("prep"), V("tr"))
+        for m in range(14):
             a, n = seg_lc(m)
-            act(V("xlc", a, a + n), V("prep", 16 * m, C), AF.Abs, 512.0, V("ccn", m, m + 1))
-        act(V("pwb"), IND(V("to"), V("cl", 0, 1)))
-        act(V("pwf"), IND(V("to"), V("cl", 0, 1)))
-        if t == 0:
-            act(V("ex"), IND(V("px", 32, 48), V("lx")))
-        for m in range(4, -1, -1):
-            a, n = seg_lc(m)
-            ts(V("xlc", a, a + n), V("prep", 16 * m, C), V("ccb", m, m + 1), A.not_equal, 512.0, A.mult)
-        for a, b in ((720, TRI), (0, 720)):
+            if m < LCV:
+                ts(V("xlc", a, a + n), V("prep", 16 * m, C), V("ccb", m, m + 1), A.not_equal, 512.0, A.mult)
+            else:
+                act(V("xlc", a, a + n), V("prep", 16 * m, C), AF.Abs, 512.0, V("ccn", m, m + 1))
+        for m0, m1 in ((0, 1), (2, 3), (4, 6), (7, 9), (10, 13)):
+            a, b = seg_lc(m1)[0], sum(seg_lc(m0))
             scan(V("olc", a, b), V("xlc", a, b), V("klc", a, b), 0.0, A.min, A.max)
+        lb = slot("ld", 16)
+        ts(V("ld", lb, lb + 16), IND(V("olc"), V("cl", 2, 3)), -1.0, A.mult, 256.0, A.add)
+        listed(V("pwf", 0, 14), V("prep"))
+        if len(PSV) < 14:
+            ts(V("pwn", 0, 14), V("pwf", 0, 14), -512.0, A.mult)
         for m in range(14):
             a, n = seg_ps(m)
-            later.append(lambda a=a, n=n, m=m: ts(V("xps", a, a + n), V("prep", 0, n, -1), V("pwb", m, m + 1), A.not_equal, 512.0, A.mult))
-        for m0, m1 in ((0, 7), (7, 10), (10, 12), (12, 14)):
+            if m in PSV:
+                ts(V("xps", a, a + n), V("prep", 0, n, -1), V("pwf", m, m + 1), A.not_equal, 512.0, A.mult)
+            else:
+                act(V("xps", a, a + n), V("prep", 0, n, -1), AF.Abs, 512.0, V("pwn", m, m + 1))
+        for m0, m1 in PSS:
             a, b = seg_ps(m0)[0], seg_ps(m1)[0]
-            later.append(lambda a=a, b=b: scan(V("ops", a, b), V("xps", a, b), V("kps", a, b), 1000.0, A.min, A.add))
-        later.append(lambda: ts(V("pt1"), IND(V("ops"), V("cl", 4, 5)), -1.0, A.mult, 255.0, A.add))
-        later.append(lambda: tt(V("pt2"), V("pt1"), V("pwf"), A.max))
-        later.append(lambda: cp(V("lps", 2, 16), V("pt2", 0, 14)))
-        if t == 0:
-            jump_constants()
-        fill(2)
-        ts(V("ld", 0, 16), IND(V("olc"), V("cl", 2, 3)), -1.0, A.mult, 256.0, A.add)
-        fill(2)
-        gather2("ja", 64, V("idp"), "ld", 0, 14, 8)
-        fill(2)
-        gather2("jc", 64, V("ja", 64, 288), "ld", 0, 14, 8)
-        fill(2)
-        old, new = 0, 16
-        for lev in range(5):
-            gather2("ja", 64, V("jc", 64, 288), "ld", old, old + 14, old)
-            diag("eo1", "jc", 64, C)
-            fill(2 if lev < 1 else 1)
-            pickd(V("ld", new, new + 14), "eo1", 0, C)
-            fill(2 if lev < 1 else 1)
-            if t == R - 1 and lev == 0:
-                act(V("pout", 1, C), V("prep", 1, C))
-                dma("s", T.op[:], T.pout[0:128:16, :], [], [V("pout")])
-            gather2("jc", 64, V("ja", 64, 288), "ld", new, new + 14, new + 8)
-            fill(2 if lev < 1 else 1)
-            old, new = new, old
-        gather2("bot", 256, V("jc", 64, 288), "ld", old, old + 14, old + 8)
-        fill(30)
+            scan(V("ops", a, b), V("xps", a, b), V("kps", a, b), 1000.0, A.min, A.add)
+        ts(V("pt1"), IND(V("ops"), V("cl", 4, 5)), -1.0, A.mult, 255.0, A.add)
+        tt(V("pt2", 0, 14), V("pt1", 0, 14), V("pwf", 0, 14), A.max)
+        cp(V("lps", 0, 14), V("pt2", 0, 14))
+        if t == R - 1:
+            act(V("pout", 1, C), V("prep", 1, C), AF.Identity, 1.0, -1.0)
+            dma("s", T.op[:], T.pout[0:128:16, :], [], [V("pout")])
+        ja, jb = V("ja"), V("bot", 256, 480)
+        gather2("bot", 256, V("idp"), "ld", lb, 8)
+        gather2("ja", 0, jb, "ld", lb, 8)
+        a, b, held = 2, 1, 1
+        while held < C:
+            na, nb = (C - a + 15) // 16, (C - held + 15) // 16
+            if a + b >= C:
+                gather2("bot", 256, ja, "ld", lb, nb // 2, nb)
+            else:
+                gather2("bot", 256, ja, "ld", lb, B1, nb)
+                lb = new_list(V("ja", 0, 16 * na))
+                gather2("ja", 0, jb, "ld", lb, min(M1, (na + 2) // 4 * 2), na)
+            a, b, held = 2 * a + b, a, a + b
+        listed(V("lb", 0, 14), jb)
         for out, q, s in (("ph", lq, ls), ("pt", qx, sx)):
             for b in range(4):
                 mm(V(out, 512 * b, 512 * b + C), V("eq", 128 * b, 128 * b + 128), V("es", 128 * b, 128 * b + 128), q, s)
-        later.append(lambda: diag("eo3", "bot", 256, C))
-        later.append(lambda: pickd(V("lb", 0, 14), "eo3", 0, C))
-        if t == 0:
-            order_constants()
-        free = [("ja", 0), ("ja", 256), ("jc", 0), ("jc", 256)]
-
-        def table(x):
-            return V(x[0], x[1], x[1] + C)
-
-        def unpacked(k):
-            act(V("tp", C * k, C * k + C), V("ph", 512 * k, 512 * k + C))
-
-        ta = free.pop(0)
-        gather2(ta[0], ta[1], V("bot"), "lps", 2, 16, 10)
-        act(V("ot", 1, 17), IND(V("bot"), V("lps", 0, 1)))
-        a, b, m, old, new = 1, 0, 2, 0, 16
+        for b in range(4):
+            act(V("tp", C * b, C * b + C), V("ph", 512 * b, 512 * b + C))
+        ta = slot("jt", C)
+        gather2("jt", ta, V("bot"), "lps", 0, 8)
+        act(V("ot", 0, 1), V("bot", 256, 257))
+        a, b, lo = 1, 0, slot("ld", 16)
+        cp(V("ld", lo, lo + 1), V("bot", 256, 257))
+        move = {"v": cp, "a": act}
         for step in range(6):
-            co = (m + 15) // 16
-            tb = ta
+            tb = power(table(ta), lb, B2) if b else ta
+            lb = new_list(table(ta))
             if step < 5:
-                diag("eo1", ta[0], ta[1], C)
-            diag("eo2", "ot", 0, 16 * co)
+                ln = new_list(V("ot", 0, (a + 15) // 16 * 16)) if b else lo
             if b:
-                tb = free.pop(0)
-                gather2(tb[0], tb[1], table(ta), "ld", old, old + 14, old + (6 if step == 5 else 0))
-            else:
-                unpacked(0)
-                unpacked(1)
-            if m < a + b:
-                act(V("ot", a, a + 16 * ((b + 15) // 16)), IND(table(ta), V("oq", old, old + (b + 15) // 16)))
-            fill()
-            if step < 5:
-                pickd(V("ld", new, new + 14), "eo1", 0, C)
-            pickd(V("oq", new, new + co), "eo2", 0, 16 * co)
-            if step < 5:
-                fill()
-                tc = free.pop(0)
-                gather2(tc[0], tc[1], table(tb), "ld", new, new + 14, new + 6)
-                cp(V("ot", a + b, a + b + 16 * co), IND(table(tb), V("oq", new, new + co)))
-                free.extend([ta] if tb == ta else [ta, tb])
-                ta = tc
-            else:
-                gather2("ot", a + b, table(tb), "oq", new, new + co, new + 2)
-            a, b, m, old, new = 2 * a + b, a, a + b + m, new, old
-        fill(9)
-        diag("eo2", "ot", 64, 64)
-        unpacked(2)
-        unpacked(3)
-        pickd(V("oq", 0, 4), "eo2", 0, 64)
-        cp(V("ot", 163, 227), IND(table(tb), V("oq", 0, 4)))
-        scan(V("eo1", 0, C), V("ot", 1, 225, -1), V("ex", 0, C), -1.0, A.max, A.add)
-        pickd(V("ol"), "eo1", 0, C)
+                move[SEQ[0] if step < 5 else "v"](V("ot", a, a + (b + 15) // 16 * 16), IND(table(ta), V("ld", lo, lo + (b + 15) // 16)))
+            if step == 5:
+                listed(V("om"), V("ot", 0, C - HA, -1))
+                send("m", t, V("om"), lm)
+                cp(IND(V("plr"), V("om")), V("idp", HA, C))
+                ln = new_list(V("ot", 0, (a + 15) // 16 * 16))
+            ta = power(table(tb), lb, M2)
+            move[SEQ[1] if step < 5 else "v"](V("ot", a + b, a + b + (a + 15) // 16 * 16), IND(table(tb), V("ld", ln, ln + (a + 15) // 16)))
+            a, b, lo = 2 * a + b, a, ln
+        cp(V("ot", a + 32, a + 64), IND(table(ta), V("ld", lo + 2, lo + 4)))
+        cp(V("ot", a, a + 32), IND(table(ta), V("ld", lo, lo + 2)))
+        listed(V("ol"), V("ot", C - HA, C, -1))
         send("l", t, V("ol"), ll)
-        cp(IND(V("plr"), V("ol")), V("idp", 0, C))
-        act(V("rr"), IND(V("plr"), V("lb", 0, 14)))
-        diag("eo1", "plr", 0, C)
-        pickd(V("z", 56, 84, 2), "eo1", 0, C)
-        if t == 1:
-            quant(V("vq"), V("vs"), V("vt"))
-        diag("eo2", "rr", 0, C)
-        pickd(V("z", 57, 84, 2), "eo2", 0, C)
-        l, r, l4, i16, j16 = V("z", 56, 84, 2), V("z", 57, 84, 2), V("z", 28, 56, 2), V("z", 0, 28, 2), V("z", 1, 28, 2)
-        w = [V("w1", 16 * k, 16 * k + 14) for k in range(8)]
-        nv = 2 if route(T, topo, rank, t)[0] != route(T, topo, rank, t)[1] else 1
+        cp(IND(V("plr"), V("ol")), V("idp", 0, HA))
+        gather2("rr", 0, V("plr"), "lb", 0, 6)
+        i16, j16, l4, r4, l, r = [V("z", 28 * (k // 2) + k % 2, 28 * (k // 2) + 28, 2) for k in range(6)]
+        listed(l, V("plr"))
+        listed(r, V("rr"))
+        w = [V("w1", 16 * k, 16 * k + 14) for k in range(12)]
         ts(V("z", 28, 56), V("z", 56, 84), 2, A.logical_shift_right)
         ts(V("z", 0, 28), V("z", 56, 84), 4, A.logical_shift_right)
         tt(V("dd", 0, 42), V("z", 1, 84, 2), V("z", 0, 84, 2), A.subtract)
-        ts(w[0], l4, 4.0, A.mult, float(XX - HH + 4), A.add)
-        ts(w[1], j16, 1.0, A.add)
-        ts(w[2], i16, -2.0, A.mult, float(YY - HH - 2), A.add)
-        ts(w[3], V("dd", 14, 28), -1.0, A.add, 0.0, A.max)
-        tt(V("ff", 28, 42), V("dd", 14, 28), V("dd", 0, 14), A.add)
-        ts(V("ff", 14, 28), V("dd", 28, 42), 3.0, A.is_ge)
+        f16, f4 = V("ff", 0, 14), V("ff", 14, 28)
+        ts(f16, V("dd", 0, 14), 1.0, A.min)
+        ts(f4, V("dd", 28, 42), 3.0, A.is_ge)
+        tt(w[0], f16, f4, A.add)
+        ts(w[1], w[0], float(D), A.mult)
+        tt(w[2], l, w[1], A.add)
+        tt(w[3], r, w[1], A.subtract)
+        cp(V("lr", 0, 14), w[2])
+        ts(V("lr", 16, 30), w[3], float(HH), A.add)
         ts(w[4], V("dd", 28, 42), 1.0, A.min)
-        tt(w[1], w[1], j16, A.mult)
-        ts(V("ff", 0, 14), V("ff", 28, 42), 4.0, A.is_ge)
-        for b in range(nv, 4):
-            act(V("bt", b, D, 4), IND(V("tp", C * b, C * b + C), ll))
-        for b in range(nv):
-            cp(V("bt", b, D, 4), IND(V("tp", C * b, C * b + C), ll))
-        tt(w[5], V("ff", 0, 14), V("ff", 14, 28), A.add)
-        tt(V("mm", 14, 28), w[0], w[3], A.add)
-        tt(V("mm", 0, 14), w[1], w[2], A.add)
-        quant(V("fq"), V("fs"), V("bt"))
-        for b in range(4):
-            mm(V("ph", 512 * b, 512 * b + C), V("wq", 128 * b, 128 * b + 128), V("wp", 128 * b, 128 * b + 128), V("fq"), V("fs"))
-        for b in range(4):
-            act(V("tab", HH + C * b, HH + C * b + C), V("ph", 512 * b, 512 * b + C), AF.Copy, 0.03125)
-        ts(w[5], w[5], float(D), A.mult)
-        tt(V("dd", 0, 28), V("ff", 0, 28), V("mm", 0, 28), A.mult)
-        tt(w[4], w[4], l, A.add)
-        tt(w[6], l, w[5], A.add)
-        tt(w[7], r, w[5], A.subtract)
-        tt(w[3], V("dd", 0, 14), V("dd", 14, 28), A.max)
-        cp(V("lr", 0, 14), w[6])
-        ts(V("lr", 16, 30), w[7], float(HH), A.add)
-        tt(w[4], w[4], w[3], A.max)
-        for b in range(4):
-            scan(V("tab", S16 + C * b, S16 + C * b + C, -1), V("k16", 0, C), V("tab", HH + C * b, HH + C * b + C, -1), 0.0, A.add, A.max)
-            if b == 0:
-                cp(V("lr", 32, 46), w[4])
-        act(V("mseq"), IND(V("tab", S16, YY), V("lsq")))
-        scan(V("tab", S4, S16, -1), V("k4"), V("tab", HH, S4, -1), 0.0, A.add, A.max)
-        act(V("tab", XX + 1, YY, 4), V("tab", S4, S16, 4))
-        for b in range(4):
-            act(V("ga", C * b, C * b + C), IND(V("tab", HH + C * b, S16 + C * b + C), V("lr", 0, 14)))
-        scan(V("tab", P16, P4), V("k16"), V("tab", HH, S4), 0.0, A.add, A.max)
-        scan(V("tab", P4, HH), V("k4"), V("tab", HH, S4), 0.0, A.add, A.max)
-        tt(V("tab", XX + 6, YY, 16), V("tab", S4 + 4, S16, 16), V("tab", S4 + 8, S16, 16), A.max)
+        tt(w[5], w[4], l, A.add)
+        ts(w[6], l4, 3.0, A.mult, float(XX - HH), A.add)
+        tt(V("mm", 14, 28), w[6], r4, A.add)
+        ts(w[7], j16, 1.0, A.add)
+        tt(w[8], w[7], j16, A.mult)
+        ts(w[9], i16, -2.0, A.mult, float(YY - HH - 2), A.add)
+        tt(V("mm", 0, 14), w[8], w[9], A.add)
+        tt(V("de", 0, 28), V("ff", 0, 28), V("mm", 0, 28), A.mult)
+        tt(w[10], V("de", 0, 14), V("de", 14, 28), A.max)
+        tt(w[11], w[5], w[10], A.max)
+        cp(V("lr", 32, 46), w[11])
+        hop, dst = route(T, topo, rank, t)
+        skip = 16 if t else 0
+        for k, (c0, c1, lst) in enumerate(((HA, C, lm), (0, HA, ll))):
+            for b in range(4):
+                move["v" if b in BV[hop != dst][k] else "a"](V("bt", 512 * k + b, 512 * k + 4 * (c1 - c0), 4), IND(V("tp", C * b, C * b + C), lst))
+            fq, fs = V("fq", 128 * k, 128 * k + 128), V("fs", 128 * k, 128 * k + 128)
+            quant(fq, fs, V("bt", 512 * k, 512 * k + 512))
+            for b in range(4):
+                mm(V("ph", 512 * b, 512 * b + 128), V("wq", 128 * b, 128 * b + 128), V("wp", 128 * b, 128 * b + 128), fq, fs)
+                act(V("tab", HH + C * b + c0, HH + C * b + c1), V("ph", 512 * b, 512 * b + c1 - c0), AF.Copy, 0.03125)
+        for to, resets, s, c0, c1 in ((S16, "k16", -1, 0, C - skip), (S4, "k4", -1, 0, C), (P16, "k16", 1, skip, C), (P4, "k4", 1, 0, C)):
+            if to in WHOLE[hop != dst]:
+                runs = [(c0, D - C + c1)]
+            else:
+                runs = [(C * b + HA, C * b + c1) for b in range(4)] + [(C * b + c0, C * b + HA) for b in range(4)]
+            for c2, c3 in runs:
+                scan(V("tab", to + c2, to + c3, s), V(resets, 0, c3 - c2), V("tab", HH + c2, HH + c3, s), 0.0, A.add, A.max)
+        act(V("mseq"), IND(V("tab", S16, XX + 1), V("lsq")))
+        act(V("tab", XX + 2, YY - 4, 4), V("tab", S4 + 4, S16, 4))
+        tt(V("tab", XX + 3, YY, 16), V("tab", S4 + 4, S16, 16), V("tab", S4 + 8, S16, 16), A.max)
         for b in range(4):
             scan(V("tab", YY + C * b, YY + C * b + 192, 2), V("ksq"), V("mseq", 96 * b, 96 * b + 96), 0.0, A.add, A.max)
         for b in range(4):
-            tt(V("gb", C * b, C * b + C), IND(V("tab", C * b, HH + C * b + C), V("lr", 16, 30)), V("ga", C * b, C * b + C), A.max)
-        for b in range(4):
-            tt(V("gm", C * b, C * b + C), IND(V("tab", HH + C * b, YY + C * b + C), V("lr", 32, 46)), V("gb", C * b, C * b + C), A.max)
-        for b in range(4):
-            tt(V("xs", b, D, 4), V("gm", C * b, C * b + C), V("pt", 512 * b, 512 * b + C), A.add)
+            looks = [IND(V("tab", HH + C * b, S16 + C * b + C), V("lr", 0, 14)),
+                     IND(V("tab", C * b, HH + C * b + C), V("lr", 16, 30)),
+                     IND(V("tab", HH + C * b, YY + C * b + C), V("lr", 32, 46))]
+            if b < 4 - NB:
+                ga, gb, gm = [V(x, C * b, C * b + C) for x in ("ga", "gb", "gm")]
+                act(ga, looks[0])
+                tt(gb, looks[1], ga, A.max)
+                tt(gm, looks[2], gb, A.max)
+            else:
+                o = 3 * C * (3 - b)
+                for k in range(3):
+                    act(V("g3", o + k, o + 3 * C, 3), looks[k])
+                scan(V("o3", o, o + 3 * C), V("k3"), V("g3", o, o + 3 * C), 0.0, A.add, A.max)
+                gm = V("o3", o + 2, o + 3 * C, 3)
+            tt(V("xs", b, D, 4), gm, V("pt", 512 * b, 512 * b + C), A.add)
 
     qx, sx = V("qx%d" % R), V("sx%d" % R)
     quant(qx, sx, V("xs"))
     mm(V("ph", 0, C), V("vq"), V("vs"), qx, sx)
-    dma("s", T.oc[:], qx[0].bitcast(dt.uint8), [], [qx])
     cp(V("yo"), V("ph", 0, C))
-    dma("a", T.osc[0:4, :], T["sx%d" % R][0:4, :], [], [sx])
-    dma("a", T.osc[4:8, :], T["sx%d" % R][32:36, :], [], [sx])
+    dma("s", T.oc[:], qx[0].bitcast(dt.uint8), [], [qx])
     dma("s", T.y[:], T.yo[:], [], [V("yo")])
-    dma("a", T.osc[8:12, :], T["sx%d" % R][64:68, :], [], [sx])
-    dma("a", T.osc[12:16, :], T["sx%d" % R][96:100, :], [], [sx])
+    for k in range(4):
+        dma("a", T.osc[4 * k:4 * k + 4, :], T["sx%d" % R][32 * k:32 * k + 4, :], [], [sx])
+
+    known = {e: {} for e in Q}
+    done, clock, totals = {}, {}, {}
+
+    def need(e, ev):
+        s, n = ev
+        if known[e].get(s, 0) >= n:
+            return
+        Q[e].wait_ge(T.sem[s], n)
+        for s2, n2 in clock[ev].items():
+            if known[e].get(s2, 0) < n2:
+                known[e][s2] = n2
+
+    for k in place(calls):
+        c = calls[k]
+        e = c["queue"]
+        ev = c["sem"] or ("e" + e, totals.get("e" + e, 0) + 1)
+        if e:
+            wants = {}
+            for j in c["after"]:
+                wants[done[j][0]] = max(wants.get(done[j][0], 0), done[j][1])
+            for s in sorted(wants, key=lambda s: (s == "e" + e, s)):
+                need(e, (s, wants[s]))
+            issued = c["call"]()
+            if ev[0][0] != "s":
+                issued.then_inc(T.sem[ev[0]], 16 if c["sem"] else 1)
+        done[k] = ev
+        clock[ev] = dict(known[e]) if e else {}
+        clock[ev][ev[0]] = ev[1]
+        totals[ev[0]] = ev[1]
     for s in totals:
         need("g", (s, totals[s]))

from concourse.mybir import dt, AluOpType, AxisListType, ActivationFunctionType

C, R = 224, 3
D = 4 * C
HA = 128
TRI = 1680
BIG = 1.0e29
MAGIC = 12582912.0
P16, P4, HH, S4, S16, XX, YY = [k * D for k in range(7)]
TABW = 7 * D + 32
SLOTS = 8

CYCLE, WAKE, LOCAL, REMOTE = 0.87, 200.0, 2000.0, 1600.0
TURNS, STRETCH = 900, 6000.0
PSV = range(14)
WHOLE = ((P16, P4, S4), (P4, P16))
B1, B2, M1, M2 = 0, 0, 8, 8
SEQ = "aa"
BV = (((2, 3), ()), ((2, 3), (3,)))
NB = 2
LCV = 5
PSS = ((0, 5), (5, 7), (7, 9), (9, 10), (10, 11), (11, 12), (12, 13), (13, 14))

BF, F32, I32, U16, X4, U8 = "bfloat16", "float32", "int32", "uint16", "float8_e4m3fn_x4", "uint8"
SCRATCH = {}


def _sb(name, n, t):
    SCRATCH[name] = ("sbuf", [128, n], t)


for _n, _w, _t in [
    ("xt", D, BF), ("xs", D, BF), ("ut", 512, BF), ("vt", 512, BF), ("ez", 528, BF), ("eo", 528, BF),
    ("eq", 512, X4), ("es", 512, U8), ("uq", 128, X4), ("us", 128, U8), ("vq", 128, X4), ("vs", 128, U8),
    ("wq", 512, X4), ("wp", 512, U8), ("fq", 256, X4), ("fs", 256, U8), ("tp", D, BF), ("bt", 1024, BF),
    ("idp", 272, BF), ("lx", 16, U16), ("px", 48, BF), ("ci", 16, I32), ("cf", 16, F32), ("cg", 16, F32), ("cl", 8, U16),
    ("wtb", 16, F32), ("wtm", 16, F32), ("wtn", 16, F32), ("thr", 2, F32), ("jb", 32, F32), ("d0", C, BF), ("rm", C, BF),
    ("zf", C, BF), ("tt", C, BF), ("to", C, BF), ("tr", C, BF), ("pwf", 16, F32),
    ("prep", C, BF), ("pout", C, F32), ("ccb", 16, BF), ("ccn", 16, F32), ("pat", 16, BF), ("pbk", 16, BF), ("pb2", 16, BF),
    ("klc", TRI, BF), ("kps", TRI, BF), ("xlc", TRI, BF), ("xps", TRI, BF), ("olc", TRI, BF), ("ops", TRI, BF),
    ("ex", 256, BF), ("eb", SLOTS * C, BF), ("jt", SLOTS * C, BF), ("ld", SLOTS * 16, U16),
    ("lps", 16, U16), ("pt1", 16, F32), ("pt2", 16, F32),
    ("bot", 480, BF), ("om", (C - HA) // 16, U16), ("ol", HA // 16, U16), ("ot", 240, BF), ("lb", 16, U16), ("plr", C, BF), ("rr", C, BF),
    ("z", 96, I32), ("dd", 48, I32), ("de", 32, I32), ("ff", 48, I32), ("mm", 48, I32), ("w1", 192, I32), ("lr", 48, U16),
    ("tab", TABW, F32), ("k4", D, F32), ("k16", D, F32), ("sq", 96, BF), ("ksq", 96, F32), ("lsq", 24, U16),
    ("mseq", 384, F32), ("ga", D, F32), ("gb", D, F32), ("gm", D, F32), ("yo", C, F32),
    ("k3", 3 * C, F32), ("g3", 3 * D, F32), ("o3", 3 * D, F32), ("ja", C, BF), ("pwn", 16, F32),
]:
    _sb(_n, _w, _t)
for _k in range(R + 1):
    _sb("qx%d" % _k, C, X4)
    _sb("sx%d" % _k, C, U8)
for _k in range(R):
    _sb("lq%d" % _k, C, X4)
    _sb("ls%d" % _k, C, U8)
    _sb("lm%d" % _k, (C - HA) // 16, U16)
    _sb("ll%d" % _k, HA // 16, U16)
SCRATCH["pt"] = ("psum", [128, 2048], F32)
SCRATCH["ph"] = ("psum", [128, 2048], F32)

SEMAPHORES = ["ev", "ea", "et", "eg"] + ["dm%d" % k for k in range(16)] + \
    [a + b + str(k) for a in "as" for b in "qsml" for k in range(R)]


def count(mask):
    return bin(mask).count("1")


def route(T, topo, rank, t):
    src, dst = T.cores[rank], T.cores[rank ^ (1 << t)]
    if topo.may_write(src, dst):
        return dst, dst
    can = [c for c in topo.cores_of(src) if T.rank_of(c) is None and topo.may_write(c, dst)]
    return [c for c in can if topo.die(c) == topo.die(src)][0], dst


def hand_on(g, core, T, topo):
    for t in range(R):
        for r in range(len(T.cores)):
            hop, dst = route(T, topo, r, t)
            if hop != core or hop == dst:
                continue
            n_in = count(topo.mask(T.cores[r], core))
            rid, pid = topo.addr(dst, core)
            m = topo.mask(core, dst)
            for k in "qsml":
                ap = T["l%s%d" % (k, t)][:]
                if k == "q":
                    ap = ap.bitcast(dt.uint8)
                g.wait_ge(T.sem["a%s%d" % (k, t)], n_in)
                g.remote_dma(ap, ap, T.sem["a%s%d" % (k, t)], T.sem["s%s%d" % (k, t)], pid, rid, m)
            for k in "qsml":
                g.wait_ge(T.sem["s%s%d" % (k, t)], count(m))


def lay(calls, order, before):
    start, busy = [0.0] * len(calls), {}
    for k in order:
        queue, time, hold = calls[k]
        at = 0.0
        for j in before[k]:
            at = max(at, start[j] + calls[j][1] + WAKE)
        if queue:
            taken = busy.setdefault(queue, [])
            i = len(taken)
            while i and taken[i - 1][1] > at:
                i -= 1
            while i < len(taken) and at + hold > taken[i][0]:
                at = max(at, taken[i][1])
                i += 1
            taken.insert(i, (at, at + hold))
        start[k] = at
    return start


PLACED = {}


def place(calls):
    key = tuple((c["queue"], c["time"], c["hold"]) for c in calls)
    if key in PLACED:
        return PLACED[key]
    n = len(calls)
    before = [sorted(c["after"]) for c in calls]
    behind = [[] for c in calls]
    chain = [c["time"] for c in calls]
    for k in range(n - 1, -1, -1):
        for j in before[k]:
            behind[j].append(k)
            chain[j] = max(chain[j], key[j][1] + WAKE + chain[k])

    def tighten(rank, turns):
        best = None
        for turn in range(turns):
            start = lay(key, sorted(range(n), key=lambda k: (rank[k], k)), before)
            end = max(start[k] + key[k][1] for k in range(n))
            if best is None or end < best[0]:
                best = (end, start)
            if turn + 1 < turns:
                back = lay(key, sorted(range(n), key=lambda k: (-start[k] - key[k][1], -k)), behind)
                rank = [-back[k] - key[k][1] for k in range(n)]
        return best

    best = tighten([-c for c in chain], 4)
    mix = 1
    for turn in range(TURNS):
        first, width = turn * 0.618034 % 1 * best[0], (450.0, 1200.0, 3000.0)[turn % 3]
        rank = list(best[1])
        for k in range(n):
            if first < rank[k] < first + STRETCH:
                mix = mix * 16807 % 2147483647
                rank[k] += width * (mix / 2147483647 - 0.5)
            for j in before[k]:
                rank[k] = max(rank[k], rank[j])
        best = min(tighten(rank, 2), best, key=lambda x: x[0])
    PLACED[key] = sorted(range(n), key=lambda k: (best[1][k], k))
    return PLACED[key]


def rank_program(g, core, T, topo):
    rank = T.rank_of(core)
    if rank is None:
        hand_on(g, core, T, topo)
        return
    A = AluOpType
    AF = ActivationFunctionType
    Q = {"v": g.vector, "a": g.scalar, "t": g.tensor, "g": g, "s": g.sync}
    calls = []
    recs = {}
    turns = {"eb": 0, "jt": 0, "ld": 0, "dm": 0}

    def V(name, a=0, b=None, s=1):
        w = SCRATCH[name][1][1]
        b = w if b is None else b
        if SCRATCH[name][0] == "psum":
            lo, hi = a // 512 * 512, (b + 511) // 512 * 512
            m = ((1 << (hi - lo)) - 1) << lo
        elif abs(s) == 1:
            m = ((1 << (b - a)) - 1) << a
        else:
            m = sum(1 << i for i in range(a, b, s))
        if s == -1:
            ap = T[name][:, b - 1:(a - 1 if a else None):-1]
        elif s == 1:
            ap = T[name][:, a:b]
        else:
            ap = T[name][:, a:b:s]
        return (ap, name, m, [], len(range(a, b, abs(s))))

    def IND(win, off):
        return (win[0].indirect(off[0]), win[1], win[2], [off], 16 * off[4])

    def ap(x):
        return x[0] if isinstance(x, tuple) else x

    def slot(name, width):
        turns[name] += 1
        return turns[name] % SLOTS * width

    def add(queue, writes, reads, call, time, hold=None, sem=None, more=()):
        rd = []
        for x in reads:
            if isinstance(x, tuple):
                rd.append(x)
                rd.extend(x[3])
        for x in writes:
            rd.extend(x[3])
        wr = list(writes) + [x for x in rd if SCRATCH[x[1]][0] == "psum"]
        rd = [x for x in rd if SCRATCH[x[1]][0] != "psum"]
        after = set(more)
        for x in wr:
            after.update(k for m, k, w in recs.get(x[1], []) if m & x[2])
        for x in rd:
            after.update(k for m, k, w in recs.get(x[1], []) if w and m & x[2])
        k = len(calls)
        calls.append({"queue": queue, "call": call, "time": time, "hold": time if hold is None else hold, "sem": sem, "after": after})
        for x in wr:
            recs[x[1]] = [(m & ~x[2], v, w) for m, v, w in recs.get(x[1], []) if m & ~x[2]] + [(x[2], k, True)]
        for x in rd:
            recs.setdefault(x[1], []).append((x[2], k, False))
        return k

    def op(e, out, reads, call, cycles=1.0):
        full = [x for x in [out] + reads if isinstance(x, tuple) and x[4] > 1]
        if out[3]:
            time = (60 + 3.8 * out[4]) * CYCLE
        elif reads and reads[0][3]:
            time = ((60 if e == "v" else 78) + 1.56 * out[4]) * CYCLE
        else:
            if e == "v" and all(SCRATCH[x[1]][2] in (BF, U16) for x in full):
                cycles /= 2
            time = (max(64, cycles * (reads[0] if reads else out)[4]) + 26) * CYCLE
        add(e, [out], reads, call, time)

    def dma(e, out, in_, writes, reads):
        turns["dm"] += 1
        add(e, writes, reads, lambda: Q[e].dma_start(out, in_), LOCAL, 100.0, ("dm%d" % turns["dm"], 16))

    def send(kind, t, src, land):
        hop, dst = route(T, topo, rank, t)
        rid, pid = topo.addr(hop, core)
        m = topo.mask(core, hop)
        a, b = src[0], land[0]
        if kind == "q":
            a, b = a.bitcast(dt.uint8), b.bitcast(dt.uint8)
        arrive, leave = "a%s%d" % (kind, t), "s%s%d" % (kind, t)
        time = REMOTE * (1 if kind in "ml" else 4)
        k = add("g", [], [src], lambda: g.remote_dma(b, a, T.sem[arrive], T.sem[leave], pid, rid, m), time, 100.0, (leave, count(m)))
        hop2, me = route(T, topo, rank ^ (1 << t), t)
        last = dst if hop2 == me else hop2
        add(None, [land], [], None, 1.0 if hop == dst else time, 0.0, (arrive, count(topo.mask(last, core))), [k])

    def ts(out, in0, s1, o0, s2=None, o1=None):
        if o1 is None:
            op("v", out, [in0, s1], lambda: g.vector.tensor_scalar(out[0], in0[0], ap(s1), None, o0))
        else:
            op("v", out, [in0, s1, s2], lambda: g.vector.tensor_scalar(out[0], in0[0], ap(s1), ap(s2), o0, o1))

    def tt(out, a, b, o):
        op("v", out, [a, b], lambda: g.vector.tensor_tensor(out[0], a[0], b[0], o), 1.0 if SCRATCH[b[1]][0] == "psum" else 2.0)

    def cp(out, a):
        op("v", out, [a], lambda: g.vector.tensor_copy(out[0], a[0]))

    def ms(out, c):
        op("v", out, [], lambda: g.vector.memset(out[0], c))

    def scan(out, d0, d1, init, o0, o1):
        op("v", out, [d0, d1], lambda: g.vector.tensor_tensor_scan(out[0], d0[0], d1[0], init, o0, o1))

    def turn(out, a):
        op("v", out, [a], lambda: g.vector.transpose(out[0], a[0]))

    def act(out, a, f=AF.Copy, scale=1.0, bias=None):
        if bias is None:
            op("a", out, [a], lambda: g.scalar.activation(out[0], a[0], f, scale=scale))
        else:
            op("a", out, [a, bias], lambda: g.scalar.activation(out[0], a[0], f, bias=ap(bias), scale=scale))

    def quant(q, s, x):
        add("v", [q, s], [x], lambda: g.vector.quantize_mx(q[0], s[0], x[0]), (14 + 0.265 * x[4]) * CYCLE)

    def mm(out, lq, ls, rq, rs):
        add("t", [out], [lq, ls, rq, rs], lambda: g.tensor.matmul_mx(out[0], lq[0], ls[0], rq[0], rs[0], True, True), 40 + 0.6 * rq[4])

    def iota(out, pat, base=0, cm=0):
        if SCRATCH[out[1]][2] == I32:
            add("g", [out], [], lambda: g.iota(out[0], pat, base, cm), (157 + 2 * out[4]) * CYCLE)
        else:
            add("g", [out], [], lambda: g.iota(out[0], pat, base, cm, allow_small_or_imprecise_dtypes=True), (157 + 2 * out[4]) * CYCLE)

    def asel(out, a, pat, cmp, fill_, base, cm):
        add("g", [out], [a], lambda: g.affine_select(out[0], a[0], pat, cmp, fill_, base, cm), (205 + 2 * out[4]) * CYCLE)

    def gather2(out, o0, win, off, c0, cv, n=14):
        if cv < n:
            act(V(out, o0 + 16 * cv, o0 + 16 * n), IND(win, V(off, c0 + cv, c0 + n)))
        if cv > 0:
            cp(V(out, o0, o0 + 16 * cv), IND(win, V(off, c0, c0 + cv)))

    def listed(out, src, *more):
        a = slot("eb", C)
        scan(V("eb", a, a + src[4]), src, V("ex", 0, src[4]), -1.0, A.max, A.add)
        ts(out, V("eb", a + 15, a + src[4], 16), 256.0, A.add, *more)

    def table(a):
        return V("jt", a, a + C)

    def power(win, lst, cv):
        a = slot("jt", C)
        gather2("jt", a, win, "ld", lst, cv)
        return a

    def new_list(src):
        a = slot("ld", 16)
        listed(V("ld", a, a + src[4] // 16), src)
        return a

    dma("s", T.xt[:], T.x[:], [V("xt")], [])
    dma("a", T.ut[:], T.u[:], [V("ut")], [])
    dma("s", T.wq[:].bitcast(dt.uint8), T.wc[:], [V("wq")], [])
    dma("s", T.wp[:], T.ws[:], [V("wp")], [])
    dma("s", T.vt[:], T.v[:], [V("vt")], [])
    quant(V("uq"), V("us"), V("ut"))
    quant(V("vq"), V("vs"), V("vt"))

    iota(V("ci", 0, 1), [[0, 1]], 0, 1)
    iota(V("idp"), [[1, 272]])
    iota(V("jb", 0, 14), [[32, 7], [0, 2]])
    ts(V("ci", 1, 2), V("ci", 0, 1), 15, A.bitwise_and)
    ts(V("ci", 2, 3), V("ci", 0, 1), 31, A.bitwise_and)
    cp(V("cf", 1, 3), V("ci", 1, 3))
    pm16, pm32 = V("cf", 1, 2), V("cf", 2, 3)
    for a, b, c in ((0, 8, -128.0), (8, 11, 0.0), (11, 12, 127.5 / 256), (12, 14, -MAGIC), (14, 15, 1.0), (15, 16, 0.0)):
        ms(V("wtb", a, b), c)
    ts(V("wtm"), V("idp", 0, 16), pm16, A.is_equal)
    tt(V("wtn"), V("wtm"), V("wtb"), A.mult)
    op("v", V("thr", 1, 2), [V("wtn")], lambda: g.vector.tensor_reduce(T.thr[:, 1:2], T.wtn[:], AxisListType.X, A.add))
    ts(V("thr", 0, 1), pm16, 7.5, A.is_gt, -BIG, A.mult)
    ms(V("d0"), 0.5)
    for k, c in ((0, 0.0), (12, 1.0), (13, -1.0), (14, 1.0)):
        ms(V("d0", k, C, 16), c)
    ts(V("d0", 11, C, 16), V("jb", 0, 14), pm32, A.add, 1.0 / 32, A.mult)
    ts(V("jb", 16, 30), V("d0", 11, C, 16), 0.0, A.is_equal, 255.0, A.mult)
    ts(V("d0", 15, C, 16), V("jb", 16, 30), 1.0, A.add)
    ms(V("rm"), 1.0)
    ms(V("rm", 15, C, 16), 0.0)
    iota(V("kps"), [[0, TRI]], -1)
    ts(V("pat"), V("idp", 0, 16), pm16, A.max)
    ts(V("pb2"), V("idp", 0, 16), pm16, A.add, 15.5, A.is_le)
    ts(V("pbk"), V("pb2"), 1025.0, A.mult, -1.0, A.add)
    ts(V("ccb", 0, 14), V("idp", 1, C, 16), pm16, A.add)
    ts(V("ccn", 0, 14), V("ccb", 0, 14), -512.0, A.mult)
    ts(V("cg", 0, 1), pm16, -1.0, A.mult, 14.0, A.add)
    ts(V("cg", 1, 2), V("cg", 0, 1), 1.0, A.max)
    ts(V("cg", 2, 3), pm16, 1.0, A.add, 14.0, A.min)
    ts(V("cg", 4, 6), V("cg", 1, 3), 1.0, A.add, 8.0, A.mult)
    tt(V("cg", 6, 8), V("cg", 4, 6), V("cg", 1, 3), A.mult)
    ts(V("cl", 2, 6, 2), V("cg", 6, 8), -1.0, A.add)

    def seg_lc(m):
        n = 14 - m
        return 8 * n * (n - 1), 16 * n

    def seg_ps(m):
        n = m + 1
        return 8 * n * (n - 1), 16 * n

    for m in range(14):
        a, n = seg_lc(m)
        if n > 16:
            act(V("klc", a + 16, a + n), V("idp", 16 * m + 16, C), AF.Identity, -1.0, 256.0)
        act(V("klc", a, a + 16), V("pat"), AF.Identity, -1.0, 256.0 - 16 * m)
        a, n = seg_ps(m)
        act(V("kps", a, a + 16), V("pbk"))
    ts(V("px", 0, 16), V("idp", 0, 16), pm16, A.is_equal, 256.0, A.mult)
    ts(V("px", 16, 32), V("idp", 0, 16), pm16, A.is_lt, -256.0, A.mult)
    tt(V("px", 32, 48), V("px", 0, 16), V("px", 16, 32), A.add)
    ts(V("px", 47, 48), V("px", 47, 48), -512.0, A.add)
    ts(V("lx"), V("idp", 0, 16), 0.0, A.mult, pm16, A.add)
    act(V("ex"), IND(V("px", 32, 48), V("lx")))
    ms(V("ot"), 0.0)
    ms(V("bt", 4 * (C - HA), 512), 0.0)
    iota(V("bot", 0, 256), [[1, 256]], -1)
    iota(V("pout", 0, 1), [[0, 1]])
    iota(V("eo"), [[0, 528]], 1)
    asel(V("ez"), V("eo"), [[1, 528]], A.is_equal, 0.0, -3, -4)
    for b in range(4):
        quant(V("eq", 128 * b, 128 * b + 128), V("es", 128 * b, 128 * b + 128), V("ez", 3 - b, 515 - b))
    iota(V("sq"), [[0, 96]], D // 16)
    for j in range(2, 14):
        a = j * (j - 1) // 2 + 1
        act(V("sq", a, a + j - 1), V("idp", 1, j, -1))
    iota(V("tab", YY, TABW), [[0, D + 32]])
    asel(V("tab", XX, YY), V("tab", YY, YY + D), [[0, D]], A.is_gt, -BIG, 0, 0)
    for name, n in (("k16", 16), ("k4", 4), ("k3", 3)):
        w = SCRATCH[name][1][1]
        asel(V(name), V("tab", YY, YY + w), [[0, w // n], [1, n]], A.is_gt, -BIG, 0, 0)
    ts(V("ksq"), V("sq"), D / 16, A.is_equal, -BIG, A.mult)
    listed(V("pt1", 0, 6), V("sq"), 16.0, A.mult)
    for b in range(4):
        ts(V("lsq", 6 * b, 6 * b + 6), V("pt1", 0, 6), float(C * b), A.add, float(D), A.min)

    for t in range(R):
        qx, sx = V("qx%d" % t), V("sx%d" % t)
        lq, ls, lm, ll = [V("l%s%d" % (k, t)) for k in "qsml"]
        quant(qx, sx, V("xt" if t == 0 else "xs"))
        mm(V("ph", 0, C), V("uq"), V("us"), qx, sx)
        send("q", t, qx, lq)
        send("s", t, sx, ls)
        ts(V("zf"), V("ph", 0, C), V("thr", 0, 1), A.is_gt, V("thr", 1, 2), A.mult)
        turn(V("tt"), V("zf"))
        scan(V("to"), V("d0"), V("tt"), 0.0, A.mult, A.add)
        scan(V("tr", 0, C, -1), V("rm", 0, C, -1), V("to", 0, C, -1), 0.0, A.mult, A.max)
        turn(V("prep"), V("tr"))
        for m in range(14):
            a, n = seg_lc(m)
            if m < LCV:
                ts(V("xlc", a, a + n), V("prep", 16 * m, C), V("ccb", m, m + 1), A.not_equal, 512.0, A.mult)
            else:
                act(V("xlc", a, a + n), V("prep", 16 * m, C), AF.Abs, 512.0, V("ccn", m, m + 1))
        for m0, m1 in ((0, 1), (2, 3), (4, 6), (7, 9), (10, 13)):
            a, b = seg_lc(m1)[0], sum(seg_lc(m0))
            scan(V("olc", a, b), V("xlc", a, b), V("klc", a, b), 0.0, A.min, A.max)
        lb = slot("ld", 16)
        ts(V("ld", lb, lb + 16), IND(V("olc"), V("cl", 2, 3)), -1.0, A.mult, 256.0, A.add)
        listed(V("pwf", 0, 14), V("prep"))
        if len(PSV) < 14:
            ts(V("pwn", 0, 14), V("pwf", 0, 14), -512.0, A.mult)
        for m in range(14):
            a, n = seg_ps(m)
            if m in PSV:
                ts(V("xps", a, a + n), V("prep", 0, n, -1), V("pwf", m, m + 1), A.not_equal, 512.0, A.mult)
            else:
                act(V("xps", a, a + n), V("prep", 0, n, -1), AF.Abs, 512.0, V("pwn", m, m + 1))
        for m0, m1 in PSS:
            a, b = seg_ps(m0)[0], seg_ps(m1)[0]
            scan(V("ops", a, b), V("xps", a, b), V("kps", a, b), 1000.0, A.min, A.add)
        ts(V("pt1"), IND(V("ops"), V("cl", 4, 5)), -1.0, A.mult, 255.0, A.add)
        tt(V("pt2", 0, 14), V("pt1", 0, 14), V("pwf", 0, 14), A.max)
        cp(V("lps", 0, 14), V("pt2", 0, 14))
        if t == R - 1:
            act(V("pout", 1, C), V("prep", 1, C), AF.Identity, 1.0, -1.0)
            dma("s", T.op[:], T.pout[0:128:16, :], [], [V("pout")])
        ja, jb = V("ja"), V("bot", 256, 480)
        gather2("bot", 256, V("idp"), "ld", lb, 8)
        gather2("ja", 0, jb, "ld", lb, 8)
        a, b, held = 2, 1, 1
        while held < C:
            na, nb = (C - a + 15) // 16, (C - held + 15) // 16
            if a + b >= C:
                gather2("bot", 256, ja, "ld", lb, nb // 2, nb)
            else:
                gather2("bot", 256, ja, "ld", lb, B1, nb)
                lb = new_list(V("ja", 0, 16 * na))
                gather2("ja", 0, jb, "ld", lb, min(M1, (na + 2) // 4 * 2), na)
            a, b, held = 2 * a + b, a, a + b
        listed(V("lb", 0, 14), jb)
        for out, q, s in (("ph", lq, ls), ("pt", qx, sx)):
            for b in range(4):
                mm(V(out, 512 * b, 512 * b + C), V("eq", 128 * b, 128 * b + 128), V("es", 128 * b, 128 * b + 128), q, s)
        for b in range(4):
            act(V("tp", C * b, C * b + C), V("ph", 512 * b, 512 * b + C))
        ta = slot("jt", C)
        gather2("jt", ta, V("bot"), "lps", 0, 8)
        act(V("ot", 0, 1), V("bot", 256, 257))
        a, b, lo = 1, 0, slot("ld", 16)
        cp(V("ld", lo, lo + 1), V("bot", 256, 257))
        move = {"v": cp, "a": act}
        for step in range(6):
            tb = power(table(ta), lb, B2) if b else ta
            lb = new_list(table(ta))
            if step < 5:
                ln = new_list(V("ot", 0, (a + 15) // 16 * 16)) if b else lo
            if b:
                move[SEQ[0] if step < 5 else "v"](V("ot", a, a + (b + 15) // 16 * 16), IND(table(ta), V("ld", lo, lo + (b + 15) // 16)))
            if step == 5:
                listed(V("om"), V("ot", 0, C - HA, -1))
                send("m", t, V("om"), lm)
                cp(IND(V("plr"), V("om")), V("idp", HA, C))
                ln = new_list(V("ot", 0, (a + 15) // 16 * 16))
            ta = power(table(tb), lb, M2)
            move[SEQ[1] if step < 5 else "v"](V("ot", a + b, a + b + (a + 15) // 16 * 16), IND(table(tb), V("ld", ln, ln + (a + 15) // 16)))
            a, b, lo = 2 * a + b, a, ln
        cp(V("ot", a + 32, a + 64), IND(table(ta), V("ld", lo + 2, lo + 4)))
        cp(V("ot", a, a + 32), IND(table(ta), V("ld", lo, lo + 2)))
        listed(V("ol"), V("ot", C - HA, C, -1))
        send("l", t, V("ol"), ll)
        cp(IND(V("plr"), V("ol")), V("idp", 0, HA))
        gather2("rr", 0, V("plr"), "lb", 0, 6)
        i16, j16, l4, r4, l, r = [V("z", 28 * (k // 2) + k % 2, 28 * (k // 2) + 28, 2) for k in range(6)]
        listed(l, V("plr"))
        listed(r, V("rr"))
        w = [V("w1", 16 * k, 16 * k + 14) for k in range(12)]
        ts(V("z", 28, 56), V("z", 56, 84), 2, A.logical_shift_right)
        ts(V("z", 0, 28), V("z", 56, 84), 4, A.logical_shift_right)
        tt(V("dd", 0, 42), V("z", 1, 84, 2), V("z", 0, 84, 2), A.subtract)
        f16, f4 = V("ff", 0, 14), V("ff", 14, 28)
        ts(f16, V("dd", 0, 14), 1.0, A.min)
        ts(f4, V("dd", 28, 42), 3.0, A.is_ge)
        tt(w[0], f16, f4, A.add)
        ts(w[1], w[0], float(D), A.mult)
        tt(w[2], l, w[1], A.add)
        tt(w[3], r, w[1], A.subtract)
        cp(V("lr", 0, 14), w[2])
        ts(V("lr", 16, 30), w[3], float(HH), A.add)
        ts(w[4], V("dd", 28, 42), 1.0, A.min)
        tt(w[5], w[4], l, A.add)
        ts(w[6], l4, 3.0, A.mult, float(XX - HH), A.add)
        tt(V("mm", 14, 28), w[6], r4, A.add)
        ts(w[7], j16, 1.0, A.add)
        tt(w[8], w[7], j16, A.mult)
        ts(w[9], i16, -2.0, A.mult, float(YY - HH - 2), A.add)
        tt(V("mm", 0, 14), w[8], w[9], A.add)
        tt(V("de", 0, 28), V("ff", 0, 28), V("mm", 0, 28), A.mult)
        tt(w[10], V("de", 0, 14), V("de", 14, 28), A.max)
        tt(w[11], w[5], w[10], A.max)
        cp(V("lr", 32, 46), w[11])
        hop, dst = route(T, topo, rank, t)
        skip = 16 if t else 0
        for k, (c0, c1, lst) in enumerate(((HA, C, lm), (0, HA, ll))):
            for b in range(4):
                move["v" if b in BV[hop != dst][k] else "a"](V("bt", 512 * k + b, 512 * k + 4 * (c1 - c0), 4), IND(V("tp", C * b, C * b + C), lst))
            fq, fs = V("fq", 128 * k, 128 * k + 128), V("fs", 128 * k, 128 * k + 128)
            quant(fq, fs, V("bt", 512 * k, 512 * k + 512))
            for b in range(4):
                mm(V("ph", 512 * b, 512 * b + 128), V("wq", 128 * b, 128 * b + 128), V("wp", 128 * b, 128 * b + 128), fq, fs)
                act(V("tab", HH + C * b + c0, HH + C * b + c1), V("ph", 512 * b, 512 * b + c1 - c0), AF.Copy, 0.03125)
        for to, resets, s, c0, c1 in ((S16, "k16", -1, 0, C - skip), (S4, "k4", -1, 0, C), (P16, "k16", 1, skip, C), (P4, "k4", 1, 0, C)):
            if to in WHOLE[hop != dst]:
                runs = [(c0, D - C + c1)]
            else:
                runs = [(C * b + HA, C * b + c1) for b in range(4)] + [(C * b + c0, C * b + HA) for b in range(4)]
            for c2, c3 in runs:
                scan(V("tab", to + c2, to + c3, s), V(resets, 0, c3 - c2), V("tab", HH + c2, HH + c3, s), 0.0, A.add, A.max)
        act(V("mseq"), IND(V("tab", S16, XX + 1), V("lsq")))
        act(V("tab", XX + 2, YY - 4, 4), V("tab", S4 + 4, S16, 4))
        tt(V("tab", XX + 3, YY, 16), V("tab", S4 + 4, S16, 16), V("tab", S4 + 8, S16, 16), A.max)
        for b in range(4):
            scan(V("tab", YY + C * b, YY + C * b + 192, 2), V("ksq"), V("mseq", 96 * b, 96 * b + 96), 0.0, A.add, A.max)
        for b in range(4):
            looks = [IND(V("tab", HH + C * b, S16 + C * b + C), V("lr", 0, 14)),
                     IND(V("tab", C * b, HH + C * b + C), V("lr", 16, 30)),
                     IND(V("tab", HH + C * b, YY + C * b + C), V("lr", 32, 46))]
            if b < 4 - NB:
                ga, gb, gm = [V(x, C * b, C * b + C) for x in ("ga", "gb", "gm")]
                act(ga, looks[0])
                tt(gb, looks[1], ga, A.max)
                tt(gm, looks[2], gb, A.max)
            else:
                o = 3 * C * (3 - b)
                for k in range(3):
                    act(V("g3", o + k, o + 3 * C, 3), looks[k])
                scan(V("o3", o, o + 3 * C), V("k3"), V("g3", o, o + 3 * C), 0.0, A.add, A.max)
                gm = V("o3", o + 2, o + 3 * C, 3)
            tt(V("xs", b, D, 4), gm, V("pt", 512 * b, 512 * b + C), A.add)

    qx, sx = V("qx%d" % R), V("sx%d" % R)
    quant(qx, sx, V("xs"))
    mm(V("ph", 0, C), V("vq"), V("vs"), qx, sx)
    cp(V("yo"), V("ph", 0, C))
    dma("s", T.oc[:], qx[0].bitcast(dt.uint8), [], [qx])
    dma("s", T.y[:], T.yo[:], [], [V("yo")])
    for k in range(4):
        dma("a", T.osc[4 * k:4 * k + 4, :], T["sx%d" % R][32 * k:32 * k + 4, :], [], [sx])

    known = {e: {} for e in Q}
    done, clock, totals = {}, {}, {}

    def need(e, ev):
        s, n = ev
        if known[e].get(s, 0) >= n:
            return
        Q[e].wait_ge(T.sem[s], n)
        for s2, n2 in clock[ev].items():
            if known[e].get(s2, 0) < n2:
                known[e][s2] = n2

    for k in place(calls):
        c = calls[k]
        e = c["queue"]
        ev = c["sem"] or ("e" + e, totals.get("e" + e, 0) + 1)
        if e:
            wants = {}
            for j in c["after"]:
                wants[done[j][0]] = max(wants.get(done[j][0], 0), done[j][1])
            for s in sorted(wants, key=lambda s: (s == "e" + e, s)):
                need(e, (s, wants[s]))
            issued = c["call"]()
            if ev[0][0] != "s":
                issued.then_inc(T.sem[ev[0]], 16 if c["sem"] else 1)
        done[k] = ev
        clock[ev] = dict(known[e]) if e else {}
        clock[ev][ev[0]] = ev[1]
        totals[ev[0]] = ev[1]
    for s in totals:
        need("g", (s, totals[s]))
